import numpy as np
import ml_dtypes


def mxq(x, axis, fmt="e4m3"):
    dtype, down = {"e4m3": (ml_dtypes.float8_e4m3fn, 7), "e5m2": (ml_dtypes.float8_e5m2, 14)}[fmt]
    v = np.moveaxis(np.asarray(x, np.float32).astype(ml_dtypes.bfloat16).astype(np.float64), axis, -1)
    blocks = v.reshape(v.shape[:-1] + (-1, 32))
    amax = np.abs(blocks).max(-1, keepdims=True)
    byte = np.maximum(np.where(amax > 0, np.frexp(amax)[1] - 1 + 127, 0) - down, 1)
    scale = np.exp2(byte - 127.0)
    codes = (blocks / scale).astype(np.float32).astype(dtype).astype(np.float64)
    return np.moveaxis((codes * scale).reshape(v.shape), -1, axis)


WIDE = False


def mx_kscale(k):
    if not WIDE:
        return np.ones(k)
    levels = np.array([10, -10, 5, -5, 0])
    if k % 512:
        return np.exp2(np.random.permutation(np.resize(levels, k // 32))).repeat(32)
    a = np.empty((k // 512, 16))
    for p in range(k // 512):
        a[p, :8] = np.random.permutation(np.resize(levels, 8))
        for g in range(8):
            far = levels[np.abs(levels - a[p, g]) >= 10]
            a[p, g + 8] = far[np.random.randint(len(far))]
    return np.exp2(a.ravel()).repeat(32)


def f64(x):
    return np.asarray(x).astype(np.float64)


def striped(idx):
    return np.tile(idx.reshape(-1, 16).T, (8, 1)).astype(np.uint16)


def unstriped(offs):
    return offs[:16].T.reshape(-1).astype(np.int64)


def sigmoid(v):
    return 1.0 / (1.0 + np.exp(-np.maximum(v, -700.0)))


K, T, S, N = 512, 1024, 512, 128


def setup_inputs():
    n = np.random.standard_normal
    s = mx_kscale(K)[:, None]
    return {
        "xT": (n((K, T)) * s).astype(np.float32),
        "side": n((N, T)).astype(np.float32),
        "w1": (n((K, N)) / np.sqrt(K) / s).astype(np.float32),
        "offs": striped(np.random.permutation(T)[:S]),
    }


def reference(xT, side, w1, offs):
    xq = mxq(f64(xT)[:, unstriped(offs)], 0, "e4m3")
    y = mxq(f64(w1), 0, "e4m3").T @ xq
    g = f64(side)[:, unstriped(offs)]
    return y * sigmoid(g)

@@ -1,0 +1,106 @@
+from contextlib import ExitStack
+
+import concourse.mybir as mybir
+
+K, T, S, N = 512, 1024, 512, 128
+FLOPS = 2 * K * S * N
+F32 = mybir.dt.float32
+BF16 = mybir.dt.bfloat16
+U32 = mybir.dt.uint32
+U16 = mybir.dt.uint16
+U8 = mybir.dt.uint8
+FP8X4 = mybir.dt.float8_e4m3fn_x4
+ACT = mybir.ActivationFunctionType
+P = 128
+
+
+def tile_picked_sidegate_sigmoid_l_kernel(tc, xT, side, w1, offs, out):
+    nc = tc.nc
+    with ExitStack() as ctx:
+        pool = ctx.enter_context(tc.tile_pool(name="pool", bufs=1))
+        psum = ctx.enter_context(tc.psum_pool(name="psum", bufs=1))
+        offsets = pool.tile([P, S // 16], U16, name="offsets")
+        warm_in = pool.tile([P, 8], F32, name="warm_in")
+        warm_out = pool.tile([P, 8], F32, name="warm_out")
+        nc.gpsimd.memset(warm_in[:], 0.0)
+        nc.scalar.activation(warm_out[:], warm_in[:], ACT.Sigmoid)
+
+        x_rows = xT.rearrange("(p j) t -> p j t", j=4)
+        raw = {}
+        for u in range(2):
+            for c in range(2):
+                raw[u, c] = pool.tile([P, 2, 512], F32, name=f"raw{u}{c}")
+                nc.sync.dma_start(raw[u, c][:], x_rows[:, 2 * u : 2 * u + 2, 512 * c : 512 * (c + 1)])
+                if (u, c) == (0, 0):
+                    nc.sync.dma_start(offsets[:], offs)
+        side_sb = pool.tile([P, T], F32, name="side_sb")
+        nc.sync.dma_start(side_sb[:], side)
+        w_raw = pool.tile([P, 4, N], F32, name="w_raw")
+        nc.sync.dma_start(w_raw[:], w1.rearrange("(p j) n -> p j n", j=4))
+
+        pairs = [pool.tile([P, 2 * T], BF16, name=f"pairs{u}", align_bytes=64) for u in range(2)]
+
+        def cast(copy, u, c, lo, hi):
+            dst = pairs[u][:, 2 * (512 * c + lo) : 2 * (512 * c + hi)].rearrange("p (c t) -> p c t", t=2)
+            copy(dst, raw[u, c][:, :, lo:hi].rearrange("p t c -> p c t"))
+
+        H = 256
+        got = [pool.tile([P, 2, H], U32, name=f"got{h}") for h in range(2)]
+
+        def gather(u, h):
+            nc.vector.tensor_copy(got[h][:, u, :], pairs[u][:].bitcast(U32).indirect(offsets[:, 16 * h : 16 * (h + 1)]))
+
+        cast(nc.vector.tensor_copy, 0, 0, 0, 512)
+        cast(nc.vector.tensor_copy, 0, 1, 0, 320)
+        cast(nc.scalar.copy, 0, 1, 320, 512)
+        gather(0, 0)
+        gather(0, 1)
+        cast(nc.scalar.copy, 1, 0, 0, 320)
+        cast(nc.vector.tensor_copy, 1, 0, 320, 512)
+        cast(nc.vector.tensor_copy, 1, 1, 0, 320)
+        cast(nc.scalar.copy, 1, 1, 320, 512)
+
+        xb = [pool.tile([P, 4 * H], BF16, name=f"xb{h}", align_bytes=64) for h in range(2)]
+        xc = [pool.tile([P, H], U32, name=f"xc{h}", align_bytes=64) for h in range(2)]
+        xs = [pool.tile([P, H], U8, name=f"xs{h}", align_bytes=64) for h in range(2)]
+        gate = [pool.tile([P, H], F32, name=f"gate{h}") for h in range(2)]
+        sig = [pool.tile([P, H], F32, name=f"sig{h}") for h in range(2)]
+        res = [pool.tile([P, H], F32, name=f"res{h}") for h in range(2)]
+        acc = [psum.tile([P, H], F32, name=f"acc{h}") for h in range(2)]
+        wb = pool.tile([P, 4 * N], BF16, name="wb", align_bytes=64)
+        wc = pool.tile([P, N], U32, name="wc", align_bytes=64)
+        ws = pool.tile([P, N], U8, name="ws", align_bytes=64)
+
+        def weave(h):
+            nc.scalar.copy(xb[h][:].bitcast(U32).rearrange("p (s u) -> p s u", u=2), got[h][:].rearrange("p u s -> p s u"))
+
+        def look_side(h):
+            nc.vector.tensor_copy(gate[h][:], side_sb[:].indirect(offsets[:, 16 * h : 16 * (h + 1)]))
+
+        def quant(h):
+            nc.vector.quantize_mx(out=xc[h][:].bitcast(FP8X4), scales=xs[h][:], in_=xb[h][:])
+
+        def product(h):
+            nc.tensor.matmul_mx(out=acc[h][:], lhsT=wc[:].bitcast(FP8X4), lhsT_scale=ws[:],
+                                rhs=xc[h][:].bitcast(FP8X4), rhs_scale=xs[h][:], start=True, stop=True)
+
+        def finish(h):
+            nc.vector.tensor_tensor(res[h][:], acc[h][:], sig[h][:], mybir.AluOpType.mult)
+            nc.sync.dma_start(out[:, H * h : H * (h + 1)], res[h][:])
+
+        gather(1, 0)
+        weave(0)
+        gather(1, 1)
+        weave(1)
+        look_side(0)
+        quant(0)
+        look_side(1)
+        nc.scalar.copy(wb[:].rearrange("p (c i t) -> p c t i", i=4, t=4), w_raw[:].rearrange("p t (c i) -> p c t i", i=4))
+        nc.scalar.activation(sig[0][:], gate[0][:], ACT.Sigmoid)
+        nc.scalar.activation(sig[1][:], gate[1][:], ACT.Sigmoid)
+        nc.vector.quantize_mx(out=wc[:].bitcast(FP8X4), scales=ws[:], in_=wb[:])
+        quant(1)
+        product(0)
+        product(1)
+        finish(0)
+        finish(1)

@@ -26,23 +26,24 @@ def tile_picked_sidegate_sigmoid_l_kernel(tc, xT, side, w1, offs, out):
         nc.scalar.activation(warm_out[:], warm_in[:], ACT.Sigmoid)
 
         x_rows = xT.rearrange("(p j) t -> p j t", j=4)
-        raw = {}
-        for u in range(2):
-            for c in range(2):
-                raw[u, c] = pool.tile([P, 2, 512], F32, name=f"raw{u}{c}")
-                nc.sync.dma_start(raw[u, c][:], x_rows[:, 2 * u : 2 * u + 2, 512 * c : 512 * (c + 1)])
-                if (u, c) == (0, 0):
-                    nc.sync.dma_start(offsets[:], offs)
+        chunks = [(0, 0, 512), (0, 512, 768), (0, 768, 1024), (1, 0, 512), (1, 512, 768), (1, 768, 1024)]
+        raw = []
+        for i, (u, lo, hi) in enumerate(chunks):
+            raw.append(pool.tile([P, 2, hi - lo], F32, name=f"raw{i}"))
+            nc.sync.dma_start(raw[i][:], x_rows[:, 2 * u : 2 * u + 2, lo:hi])
+            if i == 0:
+                nc.sync.dma_start(offsets[:], offs)
         side_sb = pool.tile([P, T], F32, name="side_sb")
-        nc.sync.dma_start(side_sb[:], side)
         w_raw = pool.tile([P, 4, N], F32, name="w_raw")
         nc.sync.dma_start(w_raw[:], w1.rearrange("(p j) n -> p j n", j=4))
+        nc.sync.dma_start(side_sb[:], side)
 
         pairs = [pool.tile([P, 2 * T], BF16, name=f"pairs{u}", align_bytes=64) for u in range(2)]
 
-        def cast(copy, u, c, lo, hi):
-            dst = pairs[u][:, 2 * (512 * c + lo) : 2 * (512 * c + hi)].rearrange("p (c t) -> p c t", t=2)
-            copy(dst, raw[u, c][:, :, lo:hi].rearrange("p t c -> p c t"))
+        def cast(copy, i, lo, hi):
+            u, first = chunks[i][0], chunks[i][1]
+            dst = pairs[u][:, 2 * (first + lo) : 2 * (first + hi)].rearrange("p (c t) -> p c t", t=2)
+            copy(dst, raw[i][:, :, lo:hi].rearrange("p t c -> p c t"))
 
         H = 256
         got = [pool.tile([P, 2, H], U32, name=f"got{h}") for h in range(2)]
@@ -50,57 +51,77 @@ def tile_picked_sidegate_sigmoid_l_kernel(tc, xT, side, w1, offs, out):
         def gather(u, h):
             nc.vector.tensor_copy(got[h][:, u, :], pairs[u][:].bitcast(U32).indirect(offsets[:, 16 * h : 16 * (h + 1)]))
 
-        cast(nc.vector.tensor_copy, 0, 0, 0, 512)
-        cast(nc.vector.tensor_copy, 0, 1, 0, 320)
-        cast(nc.scalar.copy, 0, 1, 320, 512)
-        gather(0, 0)
-        gather(0, 1)
-        cast(nc.scalar.copy, 1, 0, 0, 320)
-        cast(nc.vector.tensor_copy, 1, 0, 320, 512)
-        cast(nc.vector.tensor_copy, 1, 1, 0, 320)
-        cast(nc.scalar.copy, 1, 1, 320, 512)
-
         xb = [pool.tile([P, 4 * H], BF16, name=f"xb{h}", align_bytes=64) for h in range(2)]
-        xc = [pool.tile([P, H], U32, name=f"xc{h}", align_bytes=64) for h in range(2)]
-        xs = [pool.tile([P, H], U8, name=f"xs{h}", align_bytes=64) for h in range(2)]
-        gate = [pool.tile([P, H], F32, name=f"gate{h}") for h in range(2)]
-        sig = [pool.tile([P, H], F32, name=f"sig{h}") for h in range(2)]
-        res = [pool.tile([P, H], F32, name=f"res{h}") for h in range(2)]
-        acc = [psum.tile([P, H], F32, name=f"acc{h}") for h in range(2)]
+        prods = [(0, 256), (256, 384), (384, 512)]
+        xc = [pool.tile([P, b - a], U32, name=f"xc{i}", align_bytes=64) for i, (a, b) in enumerate(prods)]
+        xs = [pool.tile([P, b - a], U8, name=f"xs{i}", align_bytes=64) for i, (a, b) in enumerate(prods)]
+        acc = [psum.tile([P, b - a], F32, name=f"acc{i}") for i, (a, b) in enumerate(prods)]
         wb = pool.tile([P, 4 * N], BF16, name="wb", align_bytes=64)
         wc = pool.tile([P, N], U32, name="wc", align_bytes=64)
         ws = pool.tile([P, N], U8, name="ws", align_bytes=64)
+        pieces = [(0, 256), (256, 512)]
+        own = [pool.tile([P, b - a], F32, name=f"gate{i}") for i, (a, b) in enumerate(pieces)]
+        gate = [own[0][:], own[1][:]]
+        sig = [pool.tile([P, b - a], F32, name=f"sig{i}") for i, (a, b) in enumerate(pieces)]
+        res = [pool.tile([P, b - a], F32, name=f"res{i}") for i, (a, b) in enumerate(prods)]
 
         def weave(h):
             nc.scalar.copy(xb[h][:].bitcast(U32).rearrange("p (s u) -> p s u", u=2), got[h][:].rearrange("p u s -> p s u"))
 
-        def look_side(h):
-            nc.vector.tensor_copy(gate[h][:], side_sb[:].indirect(offsets[:, 16 * h : 16 * (h + 1)]))
+        def look_side(i):
+            a, b = pieces[i]
+            nc.vector.tensor_copy(gate[i], side_sb[:].indirect(offsets[:, a // 16 : b // 16]))
 
-        def quant(h):
-            nc.vector.quantize_mx(out=xc[h][:].bitcast(FP8X4), scales=xs[h][:], in_=xb[h][:])
+        def sigmoid(i):
+            nc.scalar.activation(sig[i][:], gate[i], ACT.Sigmoid)
+
+        def quant(i):
+            a, b = prods[i]
+            h = a // H
+            nc.vector.quantize_mx(out=xc[i][:].bitcast(FP8X4), scales=xs[i][:], in_=xb[h][:, 4 * (a - H * h) : 4 * (b - H * h)])
+
+        def cast_w(copy):
+            copy(wb[:].rearrange("p (c i t) -> p c t i", i=4, t=4), w_raw[:].rearrange("p t (c i) -> p c t i", i=4))
+
+        def quant_w():
+            nc.vector.quantize_mx(out=wc[:].bitcast(FP8X4), scales=ws[:], in_=wb[:])
 
         def product(h):
             nc.tensor.matmul_mx(out=acc[h][:], lhsT=wc[:].bitcast(FP8X4), lhsT_scale=ws[:],
                                 rhs=xc[h][:].bitcast(FP8X4), rhs_scale=xs[h][:], start=True, stop=True)
 
-        def finish(h):
-            nc.vector.tensor_tensor(res[h][:], acc[h][:], sig[h][:], mybir.AluOpType.mult)
-            nc.sync.dma_start(out[:, H * h : H * (h + 1)], res[h][:])
+        def finish(i, queue):
+            a, b = prods[i]
+            g = max(n for n, piece in enumerate(pieces) if piece[0] <= a)
+            first = pieces[g][0]
+            nc.vector.tensor_tensor(res[i][:], acc[i][:], sig[g][:, a - first : b - first], mybir.AluOpType.mult)
+            queue.dma_start(out[:, a:b], res[i][:])
 
+        V, A = nc.vector.tensor_copy, nc.scalar.copy
+        cast(V, 0, 0, 512)
+        cast(V, 1, 0, 256)
+        cast(V, 2, 0, 256)
+        gather(0, 0)
+        gather(0, 1)
+        cast(A, 3, 0, 512)
+        cast(V, 4, 0, 256)
+        cast(V, 5, 0, 256)
+        cast_w(A)
         gather(1, 0)
         weave(0)
         gather(1, 1)
         weave(1)
+        quant_w()
         look_side(0)
         quant(0)
-        look_side(1)
-        nc.scalar.copy(wb[:].rearrange("p (c i t) -> p c t i", i=4, t=4), w_raw[:].rearrange("p t (c i) -> p c t i", i=4))
-        nc.scalar.activation(sig[0][:], gate[0][:], ACT.Sigmoid)
-        nc.scalar.activation(sig[1][:], gate[1][:], ACT.Sigmoid)
-        nc.vector.quantize_mx(out=wc[:].bitcast(FP8X4), scales=ws[:], in_=wb[:])
-        quant(1)
         product(0)
+        look_side(1)
+        quant(1)
         product(1)
-        finish(0)
-        finish(1)
+        quant(2)
+        product(2)
+        sigmoid(0)
+        sigmoid(1)
+        finish(0, nc.sync)
+        finish(1, nc.sync)
+        finish(2, nc.sync)

@@ -7,6 +7,7 @@ FLOPS = 2 * K * S * N
 F32 = mybir.dt.float32
 BF16 = mybir.dt.bfloat16
 U32 = mybir.dt.uint32
+I32 = mybir.dt.int32
 U16 = mybir.dt.uint16
 U8 = mybir.dt.uint8
 FP8X4 = mybir.dt.float8_e4m3fn_x4
@@ -27,16 +28,29 @@ def tile_picked_sidegate_sigmoid_l_kernel(tc, xT, side, w1, offs, out):
 
         x_rows = xT.rearrange("(p j) t -> p j t", j=4)
         chunks = [(0, 0, 512), (0, 512, 768), (0, 768, 1024), (1, 0, 512), (1, 512, 768), (1, 768, 1024)]
-        raw = []
-        for i, (u, lo, hi) in enumerate(chunks):
-            raw.append(pool.tile([P, 2, hi - lo], F32, name=f"raw{i}"))
-            nc.sync.dma_start(raw[i][:], x_rows[:, 2 * u : 2 * u + 2, lo:hi])
-            if i == 0:
-                nc.sync.dma_start(offsets[:], offs)
+        raw = [pool.tile([P, 2, hi - lo], F32, name=f"raw{i}") for i, (u, lo, hi) in enumerate(chunks)]
         side_sb = pool.tile([P, T], F32, name="side_sb")
-        w_raw = pool.tile([P, 4, N], F32, name="w_raw")
-        nc.sync.dma_start(w_raw[:], w1.rearrange("(p j) n -> p j n", j=4))
-        nc.sync.dma_start(side_sb[:], side)
+        w_raw = pool.tile([P, 4, N], F32, name="w_raw", tag="w_raw_then_x", align_bytes=64)
+
+        def load_x(i, queue):
+            u, lo, hi = chunks[i]
+            queue.dma_start(raw[i][:], x_rows[:, 2 * u : 2 * u + 2, lo:hi])
+
+        def load_offsets():
+            nc.sync.dma_start(offsets[:], offs)
+
+        def load_w(queue):
+            queue.dma_start(w_raw[:], w1.rearrange("(p j) n -> p j n", j=4))
+
+        def load_side(queue):
+            queue.dma_start(side_sb[:], side)
+
+        load_x(0, nc.sync)
+        load_offsets()
+        for i in range(1, len(chunks)):
+            load_x(i, nc.sync)
+        load_w(nc.sync)
+        load_side(nc.sync)
 
         pairs = [pool.tile([P, 2 * T], BF16, name=f"pairs{u}", align_bytes=64) for u in range(2)]
 
@@ -45,40 +59,43 @@ def tile_picked_sidegate_sigmoid_l_kernel(tc, xT, side, w1, offs, out):
             dst = pairs[u][:, 2 * (first + lo) : 2 * (first + hi)].rearrange("p (c t) -> p c t", t=2)
             copy(dst, raw[i][:, :, lo:hi].rearrange("p t c -> p c t"))
 
-        H = 256
-        got = [pool.tile([P, 2, H], U32, name=f"got{h}") for h in range(2)]
+        def holder(spans, a):
+            return [n for n, span in enumerate(spans) if span[0] <= a < span[1]][0]
 
-        def gather(u, h):
-            nc.vector.tensor_copy(got[h][:, u, :], pairs[u][:].bitcast(U32).indirect(offsets[:, 16 * h : 16 * (h + 1)]))
+        joins = [(0, 128), (128, 256), (256, 384), (384, 512)]
+        got = pool.tile([P, 2, S], U32, name="got")
+        xb = {}
 
-        xb = [pool.tile([P, 4 * H], BF16, name=f"xb{h}", align_bytes=64) for h in range(2)]
-        prods = [(0, 256), (256, 384), (384, 512)]
-        xc = [pool.tile([P, b - a], U32, name=f"xc{i}", align_bytes=64) for i, (a, b) in enumerate(prods)]
-        xs = [pool.tile([P, b - a], U8, name=f"xs{i}", align_bytes=64) for i, (a, b) in enumerate(prods)]
+        def gather(u, a, b):
+            nc.vector.tensor_copy(got[:, u, a:b], pairs[u][:].bitcast(U32).indirect(offsets[:, a // 16 : b // 16]))
+
+        def join(copy, view, h, tag):
+            a, b = joins[h]
+            xb[h] = pool.tile([P, 4 * (b - a)], BF16, name=f"xb{h}", tag=tag, align_bytes=64)
+            copy(xb[h][:].bitcast(view).rearrange("p (s u) -> p s u", u=2), got[:].bitcast(view)[:, :, a:b].rearrange("p u s -> p s u"))
+
+        quants = [(0, 128), (128, 256), (256, 384), (384, 512)]
+        prods = [(0, 128), (128, 256), (256, 384), (384, 512)]
+        xc = [pool.tile([P, b - a], U32, name=f"xc{i}", align_bytes=64) for i, (a, b) in enumerate(quants)]
+        xs = [pool.tile([P, b - a], U8, name=f"xs{i}", align_bytes=64) for i, (a, b) in enumerate(quants)]
         acc = [psum.tile([P, b - a], F32, name=f"acc{i}") for i, (a, b) in enumerate(prods)]
-        wb = pool.tile([P, 4 * N], BF16, name="wb", align_bytes=64)
+        wb = pool.tile([P, 4 * N], BF16, name="wb", tag="w_then_x", align_bytes=64)
         wc = pool.tile([P, N], U32, name="wc", align_bytes=64)
         ws = pool.tile([P, N], U8, name="ws", align_bytes=64)
-        pieces = [(0, 256), (256, 512)]
-        own = [pool.tile([P, b - a], F32, name=f"gate{i}") for i, (a, b) in enumerate(pieces)]
-        gate = [own[0][:], own[1][:]]
+        pieces = [(0, 128), (128, 256), (256, 384), (384, 512)]
         sig = [pool.tile([P, b - a], F32, name=f"sig{i}") for i, (a, b) in enumerate(pieces)]
-        res = [pool.tile([P, b - a], F32, name=f"res{i}") for i, (a, b) in enumerate(prods)]
-
-        def weave(h):
-            nc.scalar.copy(xb[h][:].bitcast(U32).rearrange("p (s u) -> p s u", u=2), got[h][:].rearrange("p u s -> p s u"))
-
-        def look_side(i):
-            a, b = pieces[i]
-            nc.vector.tensor_copy(gate[i], side_sb[:].indirect(offsets[:, a // 16 : b // 16]))
+        stores = [(0, 128), (128, 256), (256, 384), (384, 512)]
+        res = {}
 
         def sigmoid(i):
-            nc.scalar.activation(sig[i][:], gate[i], ACT.Sigmoid)
+            a, b = pieces[i]
+            nc.scalar.activation(sig[i][:], side_sb[:].indirect(offsets[:, a // 16 : b // 16]), ACT.Sigmoid)
 
         def quant(i):
-            a, b = prods[i]
-            h = a // H
-            nc.vector.quantize_mx(out=xc[i][:].bitcast(FP8X4), scales=xs[i][:], in_=xb[h][:, 4 * (a - H * h) : 4 * (b - H * h)])
+            a, b = quants[i]
+            h = holder(joins, a)
+            first = joins[h][0]
+            nc.vector.quantize_mx(out=xc[i][:].bitcast(FP8X4), scales=xs[i][:], in_=xb[h][:, 4 * (a - first) : 4 * (b - first)])
 
         def cast_w(copy):
             copy(wb[:].rearrange("p (c i t) -> p c t i", i=4, t=4), w_raw[:].rearrange("p t (c i) -> p c t i", i=4))
@@ -86,42 +103,52 @@ def tile_picked_sidegate_sigmoid_l_kernel(tc, xT, side, w1, offs, out):
         def quant_w():
             nc.vector.quantize_mx(out=wc[:].bitcast(FP8X4), scales=ws[:], in_=wb[:])
 
-        def product(h):
-            nc.tensor.matmul_mx(out=acc[h][:], lhsT=wc[:].bitcast(FP8X4), lhsT_scale=ws[:],
-                                rhs=xc[h][:].bitcast(FP8X4), rhs_scale=xs[h][:], start=True, stop=True)
-
-        def finish(i, queue):
+        def product(i):
             a, b = prods[i]
-            g = max(n for n, piece in enumerate(pieces) if piece[0] <= a)
-            first = pieces[g][0]
-            nc.vector.tensor_tensor(res[i][:], acc[i][:], sig[g][:, a - first : b - first], mybir.AluOpType.mult)
-            queue.dma_start(out[:, a:b], res[i][:])
+            q = holder(quants, a)
+            first = quants[q][0]
+            nc.tensor.matmul_mx(out=acc[i][:], lhsT=wc[:].bitcast(FP8X4), lhsT_scale=ws[:],
+                                rhs=xc[q][:, a - first : b - first].bitcast(FP8X4), rhs_scale=xs[q][:, a - first : b - first], start=True, stop=True)
+
+        def result(s, tag):
+            a, b = stores[s]
+            res[s] = pool.tile([P, b - a], F32, name=f"res{s}", tag=tag, align_bytes=64)
+
+        def gate(i):
+            a, b = prods[i]
+            g, s = holder(pieces, a), holder(stores, a)
+            nc.vector.tensor_tensor(res[s][:, a - stores[s][0] : b - stores[s][0]], acc[i][:], sig[g][:, a - pieces[g][0] : b - pieces[g][0]], mybir.AluOpType.mult)
+
+        def store(s, queue):
+            a, b = stores[s]
+            queue.dma_start(out[:, a:b], res[s][:])
 
         V, A = nc.vector.tensor_copy, nc.scalar.copy
         cast(V, 0, 0, 512)
         cast(V, 1, 0, 256)
         cast(V, 2, 0, 256)
-        gather(0, 0)
-        gather(0, 1)
+        gather(0, 0, 512)
         cast(A, 3, 0, 512)
         cast(V, 4, 0, 256)
         cast(V, 5, 0, 256)
         cast_w(A)
-        gather(1, 0)
-        weave(0)
-        gather(1, 1)
-        weave(1)
+        gather(1, 0, 128)
+        gather(1, 128, 256)
+        gather(1, 256, 384)
+        gather(1, 384, 512)
+        join(A, U32, 0, "xb0")
+        join(A, U32, 1, "xb1")
         quant_w()
-        look_side(0)
+        join(V, I32, 2, "w_raw_then_x")
         quant(0)
         product(0)
-        look_side(1)
-        quant(1)
-        product(1)
-        quant(2)
-        product(2)
-        sigmoid(0)
-        sigmoid(1)
-        finish(0, nc.sync)
-        finish(1, nc.sync)
-        finish(2, nc.sync)
+        join(V, I32, 3, "w_then_x")
+        for i in range(1, 4):
+            quant(i)
+            product(i)
+        for i in range(4):
+            sigmoid(i)
+        for i in range(4):
+            result(i, "w_raw_then_x" if i == 0 else f"res{i}")
+            gate(i)
+            store(i, nc.sync)

@@ -27,7 +27,7 @@ def tile_picked_sidegate_sigmoid_l_kernel(tc, xT, side, w1, offs, out):
         nc.scalar.activation(warm_out[:], warm_in[:], ACT.Sigmoid)
 
         x_rows = xT.rearrange("(p j) t -> p j t", j=4)
-        chunks = [(0, 0, 512), (0, 512, 768), (0, 768, 1024), (1, 0, 512), (1, 512, 768), (1, 768, 1024)]
+        chunks = [(0, 0, 768), (0, 768, 1024), (1, 0, 512), (1, 512, 768), (1, 768, 1024)]
         raw = [pool.tile([P, 2, hi - lo], F32, name=f"raw{i}") for i, (u, lo, hi) in enumerate(chunks)]
         side_sb = pool.tile([P, T], F32, name="side_sb")
         w_raw = pool.tile([P, 4, N], F32, name="w_raw", tag="w_raw_then_x", align_bytes=64)
@@ -69,10 +69,14 @@ def tile_picked_sidegate_sigmoid_l_kernel(tc, xT, side, w1, offs, out):
         def gather(u, a, b):
             nc.vector.tensor_copy(got[:, u, a:b], pairs[u][:].bitcast(U32).indirect(offsets[:, a // 16 : b // 16]))
 
-        def join(copy, view, h, tag):
+        def operand(h, tag):
             a, b = joins[h]
             xb[h] = pool.tile([P, 4 * (b - a)], BF16, name=f"xb{h}", tag=tag, align_bytes=64)
-            copy(xb[h][:].bitcast(view).rearrange("p (s u) -> p s u", u=2), got[:].bitcast(view)[:, :, a:b].rearrange("p u s -> p s u"))
+
+        def join(copy, view, a, b):
+            h = holder(joins, a)
+            first = joins[h][0]
+            copy(xb[h][:].bitcast(view)[:, 2 * (a - first) : 2 * (b - first)].rearrange("p (s u) -> p s u", u=2), got[:].bitcast(view)[:, :, a:b].rearrange("p u s -> p s u"))
 
         quants = [(0, 128), (128, 256), (256, 384), (384, 512)]
         prods = [(0, 128), (128, 256), (256, 384), (384, 512)]
@@ -125,24 +129,29 @@ def tile_picked_sidegate_sigmoid_l_kernel(tc, xT, side, w1, offs, out):
 
         V, A = nc.vector.tensor_copy, nc.scalar.copy
         cast(V, 0, 0, 512)
+        cast(A, 0, 512, 768)
         cast(V, 1, 0, 256)
-        cast(V, 2, 0, 256)
         gather(0, 0, 512)
-        cast(A, 3, 0, 512)
-        cast(V, 4, 0, 256)
-        cast(V, 5, 0, 256)
+        cast(A, 2, 0, 512)
+        cast(V, 3, 0, 256)
+        cast(V, 4, 0, 176)
+        cast(A, 4, 176, 256)
         cast_w(A)
         gather(1, 0, 128)
         gather(1, 128, 256)
         gather(1, 256, 384)
         gather(1, 384, 512)
-        join(A, U32, 0, "xb0")
-        join(A, U32, 1, "xb1")
+        operand(0, "xb0")
+        join(A, U32, 0, 128)
+        operand(1, "xb1")
+        join(A, U32, 128, 256)
         quant_w()
-        join(V, I32, 2, "w_raw_then_x")
+        operand(2, "w_raw_then_x")
+        join(V, I32, 256, 384)
         quant(0)
         product(0)
-        join(V, I32, 3, "w_then_x")
+        operand(3, "w_then_x")
+        join(V, I32, 384, 512)
         for i in range(1, 4):
             quant(i)
             product(i)

@@ -56,8 +56,8 @@ def tile_picked_sidegate_sigmoid_l_kernel(tc, xT, side, w1, offs, out):
 
         def cast(copy, i, lo, hi):
             u, first = chunks[i][0], chunks[i][1]
-            dst = pairs[u][:, 2 * (first + lo) : 2 * (first + hi)].rearrange("p (c t) -> p c t", t=2)
-            copy(dst, raw[i][:, :, lo:hi].rearrange("p t c -> p c t"))
+            dst = pairs[u][:, 2 * (first + lo) : 2 * (first + hi)].rearrange("p (c i t) -> p c t i", i=4, t=2)
+            copy(dst, raw[i][:, :, lo:hi].rearrange("p t (c i) -> p c t i", i=4))
 
         def holder(spans, a):
             return [n for n, span in enumerate(spans) if span[0] <= a < span[1]][0]
@@ -76,7 +76,7 @@ def tile_picked_sidegate_sigmoid_l_kernel(tc, xT, side, w1, offs, out):
         def join(copy, view, a, b):
             h = holder(joins, a)
             first = joins[h][0]
-            copy(xb[h][:].bitcast(view)[:, 2 * (a - first) : 2 * (b - first)].rearrange("p (s u) -> p s u", u=2), got[:].bitcast(view)[:, :, a:b].rearrange("p u s -> p s u"))
+            copy(xb[h][:].bitcast(view)[:, 2 * (a - first) : 2 * (b - first)].rearrange("p (s i u) -> p s u i", i=2, u=2), got[:].bitcast(view)[:, :, a:b].rearrange("p u (s i) -> p s u i", i=2))
 
         quants = [(0, 128), (128, 256), (256, 384), (384, 512)]
         prods = [(0, 128), (128, 256), (256, 384), (384, 512)]

@@ -27,14 +27,11 @@ def tile_picked_sidegate_sigmoid_l_kernel(tc, xT, side, w1, offs, out):
         nc.scalar.activation(warm_out[:], warm_in[:], ACT.Sigmoid)
 
         x_rows = xT.rearrange("(p j) t -> p j t", j=4)
-        chunks = [(0, 0, 768), (0, 768, 1024), (1, 0, 512), (1, 512, 768), (1, 768, 1024)]
-        raw = [pool.tile([P, 2, hi - lo], F32, name=f"raw{i}") for i, (u, lo, hi) in enumerate(chunks)]
+        planes = [pool.tile([P, T], F32, name=f"plane{t}") for t in range(2)]
+        raw = pool.tile([P, 2 * T], F32, name="raw")
+        ranges = [(0, T + 512), (T + 512, T + 768), (T + 768, 2 * T)]
         side_sb = pool.tile([P, T], F32, name="side_sb")
         w_raw = pool.tile([P, 4, N], F32, name="w_raw", tag="w_raw_then_x", align_bytes=64)
-
-        def load_x(i, queue):
-            u, lo, hi = chunks[i]
-            queue.dma_start(raw[i][:], x_rows[:, 2 * u : 2 * u + 2, lo:hi])
 
         def load_offsets():
             nc.sync.dma_start(offsets[:], offs)
@@ -45,19 +42,19 @@ def tile_picked_sidegate_sigmoid_l_kernel(tc, xT, side, w1, offs, out):
         def load_side(queue):
             queue.dma_start(side_sb[:], side)
 
-        load_x(0, nc.sync)
+        nc.sync.dma_start(planes[0][:], x_rows[:, 0, :])
         load_offsets()
-        for i in range(1, len(chunks)):
-            load_x(i, nc.sync)
+        nc.sync.dma_start(planes[1][:], x_rows[:, 1, :])
+        x_flat = xT.rearrange("(p j) t -> p (j t)", j=4)
+        for lo, hi in ranges:
+            nc.sync.dma_start(raw[:, lo:hi], x_flat[:, 2 * T + lo : 2 * T + hi])
         load_w(nc.sync)
         load_side(nc.sync)
 
-        pairs = [pool.tile([P, 2 * T], BF16, name=f"pairs{u}", align_bytes=64) for u in range(2)]
+        pairs = pool.tile([P, 2 * T], BF16, name="pairs", align_bytes=64)
 
-        def cast(copy, i, lo, hi):
-            u, first = chunks[i][0], chunks[i][1]
-            dst = pairs[u][:, 2 * (first + lo) : 2 * (first + hi)].rearrange("p (c i t) -> p c t i", i=4, t=2)
-            copy(dst, raw[i][:, :, lo:hi].rearrange("p t (c i) -> p c t i", i=4))
+        def cast(copy, lo, hi):
+            copy(pairs[:, 2 * lo : 2 * hi].rearrange("p (c i t) -> p c t i", i=4, t=2), raw[:].rearrange("p (t c) -> p t c", t=2)[:, :, lo:hi].rearrange("p t (c i) -> p c t i", i=4))
 
         def holder(spans, a):
             return [n for n, span in enumerate(spans) if span[0] <= a < span[1]][0]
@@ -67,7 +64,7 @@ def tile_picked_sidegate_sigmoid_l_kernel(tc, xT, side, w1, offs, out):
         xb = {}
 
         def gather(u, a, b):
-            nc.vector.tensor_copy(got[:, u, a:b], pairs[u][:].bitcast(U32).indirect(offsets[:, a // 16 : b // 16]))
+            nc.vector.tensor_copy(got[:, u, a:b], pairs[:].bitcast(U32).indirect(offsets[:, a // 16 : b // 16]))
 
         def operand(h, tag):
             a, b = joins[h]
@@ -128,14 +125,14 @@ def tile_picked_sidegate_sigmoid_l_kernel(tc, xT, side, w1, offs, out):
             queue.dma_start(out[:, a:b], res[s][:])
 
         V, A = nc.vector.tensor_copy, nc.scalar.copy
-        cast(V, 0, 0, 512)
-        cast(A, 0, 512, 768)
-        cast(V, 1, 0, 256)
-        gather(0, 0, 512)
-        cast(A, 2, 0, 512)
-        cast(V, 3, 0, 256)
-        cast(V, 4, 0, 176)
-        cast(A, 4, 176, 256)
+        for t in range(2):
+            nc.vector.tensor_copy(got[:, 0, :].bitcast(BF16).rearrange("p (s e) -> p s e", e=2)[:, :, t], planes[t][:].indirect(offsets[:]))
+        cast(A, 0, 176)
+        cast(V, 176, 512)
+        cast(A, 512, 592)
+        cast(V, 592, 768)
+        cast(A, 768, 848)
+        cast(V, 848, 1024)
         cast_w(A)
         gather(1, 0, 128)
         gather(1, 128, 256)

@@ -11,8 +11,13 @@ I32 = mybir.dt.int32
 U16 = mybir.dt.uint16
 U8 = mybir.dt.uint8
 FP8X4 = mybir.dt.float8_e4m3fn_x4
-ACT = mybir.ActivationFunctionType
+SIGMOID = mybir.ActivationFunctionType.Sigmoid
 P = 128
+PIECE = 128
+PIECES = S // PIECE
+RANGES = [(0, 512), (512, 768), (768, 1024)]
+SCALAR_SHARE = [176, 80, 80]
+SCALAR_JOINS = 2
 
 
 def tile_picked_sidegate_sigmoid_l_kernel(tc, xT, side, w1, offs, out):
@@ -21,140 +26,81 @@ def tile_picked_sidegate_sigmoid_l_kernel(tc, xT, side, w1, offs, out):
         pool = ctx.enter_context(tc.tile_pool(name="pool", bufs=1))
         psum = ctx.enter_context(tc.psum_pool(name="psum", bufs=1))
         offsets = pool.tile([P, S // 16], U16, name="offsets")
+
         warm_in = pool.tile([P, 8], F32, name="warm_in")
         warm_out = pool.tile([P, 8], F32, name="warm_out")
-        nc.gpsimd.memset(warm_in[:], 0.0)
-        nc.scalar.activation(warm_out[:], warm_in[:], ACT.Sigmoid)
+        nc.vector.memset(warm_in[:], 0.0)
+        nc.scalar.activation(warm_out[:], warm_in[:], SIGMOID)
 
-        x_rows = xT.rearrange("(p j) t -> p j t", j=4)
-        planes = [pool.tile([P, T], F32, name=f"plane{t}") for t in range(2)]
-        raw = pool.tile([P, 2 * T], F32, name="raw")
-        ranges = [(0, T + 512), (T + 512, T + 768), (T + 768, 2 * T)]
+        x_rows = xT.rearrange("(p t) c -> p (t c)", t=4)
+        row = [pool.tile([P, T], F32, name=f"row{t}") for t in range(2)]
+        rows23 = pool.tile([P, 2 * T], F32, name="rows23")
         side_sb = pool.tile([P, T], F32, name="side_sb")
-        w_raw = pool.tile([P, 4, N], F32, name="w_raw", tag="w_raw_then_x", align_bytes=64)
+        w_raw = pool.tile([P, 4, N], F32, name="w_raw", tag="after_w_rounding", align_bytes=64)
+        nc.sync.dma_start(row[0][:], x_rows[:, :T])
+        nc.sync.dma_start(offsets[:], offs)
+        nc.sync.dma_start(row[1][:], x_rows[:, T : 2 * T])
+        landed = 0
+        for lo, hi in RANGES:
+            nc.sync.dma_start(rows23[:, landed : T + hi], x_rows[:, 2 * T + landed : 3 * T + hi])
+            landed = T + hi
+        nc.sync.dma_start(w_raw[:], w1.rearrange("(p t) n -> p t n", t=4))
+        nc.sync.dma_start(side_sb[:], side)
 
-        def load_offsets():
-            nc.sync.dma_start(offsets[:], offs)
+        pair1_all = pool.tile([P, 2 * T], BF16, name="pair1_all", align_bytes=64)
+        picked = pool.tile([P, 2, S], U32, name="picked")
+        x_codes = [pool.tile([P, PIECE], U32, name=f"x_codes{i}", align_bytes=64) for i in range(PIECES)]
+        x_scales = [pool.tile([P, PIECE], U8, name=f"x_scales{i}", align_bytes=64) for i in range(PIECES)]
+        acc = [psum.tile([P, PIECE], F32, name=f"acc{i}") for i in range(PIECES)]
+        w_bf16 = pool.tile([P, 4 * N], BF16, name="w_bf16", tag="after_w_quantise", align_bytes=64)
+        w_codes = pool.tile([P, N], U32, name="w_codes", align_bytes=64)
+        w_scales = pool.tile([P, N], U8, name="w_scales", align_bytes=64)
+        gate = [pool.tile([P, PIECE], F32, name=f"gate{i}") for i in range(PIECES)]
+        x_bf16 = {}
 
-        def load_w(queue):
-            queue.dma_start(w_raw[:], w1.rearrange("(p j) n -> p j n", j=4))
+        def entries(i):
+            return slice(i * PIECE, (i + 1) * PIECE)
 
-        def load_side(queue):
-            queue.dma_start(side_sb[:], side)
+        def listed(i):
+            return offsets[:, i * PIECE // 16 : (i + 1) * PIECE // 16]
 
-        nc.sync.dma_start(planes[0][:], x_rows[:, 0, :])
-        load_offsets()
-        nc.sync.dma_start(planes[1][:], x_rows[:, 1, :])
-        x_flat = xT.rearrange("(p j) t -> p (j t)", j=4)
-        for lo, hi in ranges:
-            nc.sync.dma_start(raw[:, lo:hi], x_flat[:, 2 * T + lo : 2 * T + hi])
-        load_w(nc.sync)
-        load_side(nc.sync)
+        def round_pair1(copy, lo, hi):
+            src = rows23[:].rearrange("p (t c) -> p t c", t=2)[:, :, lo:hi]
+            copy(pair1_all[:, 2 * lo : 2 * hi].rearrange("p (c i t) -> p c t i", i=4, t=2), src.rearrange("p t (c i) -> p c t i", i=4))
 
-        pairs = pool.tile([P, 2 * T], BF16, name="pairs", align_bytes=64)
-
-        def cast(copy, lo, hi):
-            copy(pairs[:, 2 * lo : 2 * hi].rearrange("p (c i t) -> p c t i", i=4, t=2), raw[:].rearrange("p (t c) -> p t c", t=2)[:, :, lo:hi].rearrange("p t (c i) -> p c t i", i=4))
-
-        def holder(spans, a):
-            return [n for n, span in enumerate(spans) if span[0] <= a < span[1]][0]
-
-        joins = [(0, 128), (128, 256), (256, 384), (384, 512)]
-        got = pool.tile([P, 2, S], U32, name="got")
-        xb = {}
-
-        def gather(u, a, b):
-            nc.vector.tensor_copy(got[:, u, a:b], pairs[:].bitcast(U32).indirect(offsets[:, a // 16 : b // 16]))
-
-        def operand(h, tag):
-            a, b = joins[h]
-            xb[h] = pool.tile([P, 4 * (b - a)], BF16, name=f"xb{h}", tag=tag, align_bytes=64)
-
-        def join(copy, view, a, b):
-            h = holder(joins, a)
-            first = joins[h][0]
-            copy(xb[h][:].bitcast(view)[:, 2 * (a - first) : 2 * (b - first)].rearrange("p (s i u) -> p s u i", i=2, u=2), got[:].bitcast(view)[:, :, a:b].rearrange("p u (s i) -> p s u i", i=2))
-
-        quants = [(0, 128), (128, 256), (256, 384), (384, 512)]
-        prods = [(0, 128), (128, 256), (256, 384), (384, 512)]
-        xc = [pool.tile([P, b - a], U32, name=f"xc{i}", align_bytes=64) for i, (a, b) in enumerate(quants)]
-        xs = [pool.tile([P, b - a], U8, name=f"xs{i}", align_bytes=64) for i, (a, b) in enumerate(quants)]
-        acc = [psum.tile([P, b - a], F32, name=f"acc{i}") for i, (a, b) in enumerate(prods)]
-        wb = pool.tile([P, 4 * N], BF16, name="wb", tag="w_then_x", align_bytes=64)
-        wc = pool.tile([P, N], U32, name="wc", align_bytes=64)
-        ws = pool.tile([P, N], U8, name="ws", align_bytes=64)
-        pieces = [(0, 128), (128, 256), (256, 384), (384, 512)]
-        sig = [pool.tile([P, b - a], F32, name=f"sig{i}") for i, (a, b) in enumerate(pieces)]
-        stores = [(0, 128), (128, 256), (256, 384), (384, 512)]
-        res = {}
-
-        def sigmoid(i):
-            a, b = pieces[i]
-            nc.scalar.activation(sig[i][:], side_sb[:].indirect(offsets[:, a // 16 : b // 16]), ACT.Sigmoid)
-
-        def quant(i):
-            a, b = quants[i]
-            h = holder(joins, a)
-            first = joins[h][0]
-            nc.vector.quantize_mx(out=xc[i][:].bitcast(FP8X4), scales=xs[i][:], in_=xb[h][:, 4 * (a - first) : 4 * (b - first)])
-
-        def cast_w(copy):
-            copy(wb[:].rearrange("p (c i t) -> p c t i", i=4, t=4), w_raw[:].rearrange("p t (c i) -> p c t i", i=4))
-
-        def quant_w():
-            nc.vector.quantize_mx(out=wc[:].bitcast(FP8X4), scales=ws[:], in_=wb[:])
+        def join(i, tag):
+            copy, view = (nc.scalar.copy, U32) if i < SCALAR_JOINS else (nc.vector.tensor_copy, I32)
+            x_bf16[i] = pool.tile([P, 4 * PIECE], BF16, name=f"x_bf16_{i}", tag=tag, align_bytes=64)
+            copy(x_bf16[i][:].bitcast(view).rearrange("p (s i u) -> p s u i", i=2, u=2), picked[:].bitcast(view)[:, :, entries(i)].rearrange("p u (s i) -> p s u i", i=2))
 
         def product(i):
-            a, b = prods[i]
-            q = holder(quants, a)
-            first = quants[q][0]
-            nc.tensor.matmul_mx(out=acc[i][:], lhsT=wc[:].bitcast(FP8X4), lhsT_scale=ws[:],
-                                rhs=xc[q][:, a - first : b - first].bitcast(FP8X4), rhs_scale=xs[q][:, a - first : b - first], start=True, stop=True)
+            nc.vector.quantize_mx(out=x_codes[i][:].bitcast(FP8X4), scales=x_scales[i][:], in_=x_bf16[i][:])
+            nc.tensor.matmul_mx(out=acc[i][:], lhsT=w_codes[:].bitcast(FP8X4), lhsT_scale=w_scales[:],
+                                rhs=x_codes[i][:].bitcast(FP8X4), rhs_scale=x_scales[i][:], start=True, stop=True)
 
-        def result(s, tag):
-            a, b = stores[s]
-            res[s] = pool.tile([P, b - a], F32, name=f"res{s}", tag=tag, align_bytes=64)
-
-        def gate(i):
-            a, b = prods[i]
-            g, s = holder(pieces, a), holder(stores, a)
-            nc.vector.tensor_tensor(res[s][:, a - stores[s][0] : b - stores[s][0]], acc[i][:], sig[g][:, a - pieces[g][0] : b - pieces[g][0]], mybir.AluOpType.mult)
-
-        def store(s, queue):
-            a, b = stores[s]
-            queue.dma_start(out[:, a:b], res[s][:])
-
-        V, A = nc.vector.tensor_copy, nc.scalar.copy
+        pair0_halves = picked[:, 0, :].bitcast(BF16).rearrange("p (s t) -> p s t", t=2)
         for t in range(2):
-            nc.vector.tensor_copy(got[:, 0, :].bitcast(BF16).rearrange("p (s e) -> p s e", e=2)[:, :, t], planes[t][:].indirect(offsets[:]))
-        cast(A, 0, 176)
-        cast(V, 176, 512)
-        cast(A, 512, 592)
-        cast(V, 592, 768)
-        cast(A, 768, 848)
-        cast(V, 848, 1024)
-        cast_w(A)
-        gather(1, 0, 128)
-        gather(1, 128, 256)
-        gather(1, 256, 384)
-        gather(1, 384, 512)
-        operand(0, "xb0")
-        join(A, U32, 0, 128)
-        operand(1, "xb1")
-        join(A, U32, 128, 256)
-        quant_w()
-        operand(2, "w_raw_then_x")
-        join(V, I32, 256, 384)
-        quant(0)
+            nc.vector.tensor_copy(pair0_halves[:, :, t], row[t][:].indirect(offsets[:]))
+
+        for (lo, hi), share in zip(RANGES, SCALAR_SHARE):
+            round_pair1(nc.scalar.copy, lo, lo + share)
+            round_pair1(nc.vector.tensor_copy, lo + share, hi)
+        nc.scalar.copy(w_bf16[:].rearrange("p (c i t) -> p c t i", i=4, t=4), w_raw[:].rearrange("p t (c i) -> p c t i", i=4))
+        for i in range(PIECES):
+            nc.vector.tensor_copy(picked[:, 1, entries(i)], pair1_all[:].bitcast(U32).indirect(listed(i)))
+
+        join(0, "x_bf16_0")
+        join(1, "x_bf16_1")
+        nc.vector.quantize_mx(out=w_codes[:].bitcast(FP8X4), scales=w_scales[:], in_=w_bf16[:])
+        join(2, "after_w_rounding")
         product(0)
-        operand(3, "w_then_x")
-        join(V, I32, 384, 512)
-        for i in range(1, 4):
-            quant(i)
+        join(3, "after_w_quantise")
+        for i in range(1, PIECES):
             product(i)
-        for i in range(4):
-            sigmoid(i)
-        for i in range(4):
-            result(i, "w_raw_then_x" if i == 0 else f"res{i}")
-            gate(i)
-            store(i, nc.sync)
+
+        for i in range(PIECES):
+            nc.scalar.activation(gate[i][:], side_sb[:].indirect(listed(i)), SIGMOID)
+        for i in range(PIECES):
+            result = pool.tile([P, PIECE], F32, name=f"result{i}", tag="after_w_rounding" if i == 0 else f"result{i}", align_bytes=64)
+            nc.vector.tensor_tensor(result[:], acc[i][:], gate[i][:], mybir.AluOpType.mult)
+            nc.sync.dma_start(out[:, entries(i)], result[:])

@@ -15,8 +15,8 @@ SIGMOID = mybir.ActivationFunctionType.Sigmoid
 P = 128
 PIECE = 128
 PIECES = S // PIECE
-RANGES = [(0, 512), (512, 768), (768, 1024)]
-SCALAR_SHARE = [176, 80, 80]
+RANGES = [(0, 384), (384, 768), (768, 1024)]
+SCALAR_SHARE = [256, 128, 128]
 SCALAR_JOINS = 2
 
 
@@ -24,6 +24,7 @@ def tile_picked_sidegate_sigmoid_l_kernel(tc, xT, side, w1, offs, out):
     nc = tc.nc
     with ExitStack() as ctx:
         pool = ctx.enter_context(tc.tile_pool(name="pool", bufs=1))
+        reused = ctx.enter_context(tc.tile_pool(name="reused", bufs=1))
         psum = ctx.enter_context(tc.psum_pool(name="psum", bufs=1))
         offsets = pool.tile([P, S // 16], U16, name="offsets")
 
@@ -36,7 +37,7 @@ def tile_picked_sidegate_sigmoid_l_kernel(tc, xT, side, w1, offs, out):
         row = [pool.tile([P, T], F32, name=f"row{t}") for t in range(2)]
         rows23 = pool.tile([P, 2 * T], F32, name="rows23")
         side_sb = pool.tile([P, T], F32, name="side_sb")
-        w_raw = pool.tile([P, 4, N], F32, name="w_raw", tag="after_w_rounding", align_bytes=64)
+        w_raw = reused.tile([P, 4, N], F32, name="w_raw", offset=0, align_bytes=64)
         nc.sync.dma_start(row[0][:], x_rows[:, :T])
         nc.sync.dma_start(offsets[:], offs)
         nc.sync.dma_start(row[1][:], x_rows[:, T : 2 * T])
@@ -52,7 +53,7 @@ def tile_picked_sidegate_sigmoid_l_kernel(tc, xT, side, w1, offs, out):
         x_codes = [pool.tile([P, PIECE], U32, name=f"x_codes{i}", align_bytes=64) for i in range(PIECES)]
         x_scales = [pool.tile([P, PIECE], U8, name=f"x_scales{i}", align_bytes=64) for i in range(PIECES)]
         acc = [psum.tile([P, PIECE], F32, name=f"acc{i}") for i in range(PIECES)]
-        w_bf16 = pool.tile([P, 4 * N], BF16, name="w_bf16", tag="after_w_quantise", align_bytes=64)
+        w_bf16 = reused.tile([P, 4 * N], BF16, name="w_bf16", offset=2048, align_bytes=64)
         w_codes = pool.tile([P, N], U32, name="w_codes", align_bytes=64)
         w_scales = pool.tile([P, N], U8, name="w_scales", align_bytes=64)
         gate = [pool.tile([P, PIECE], F32, name=f"gate{i}") for i in range(PIECES)]
@@ -68,9 +69,9 @@ def tile_picked_sidegate_sigmoid_l_kernel(tc, xT, side, w1, offs, out):
             src = rows23[:].rearrange("p (t c) -> p t c", t=2)[:, :, lo:hi]
             copy(pair1_all[:, 2 * lo : 2 * hi].rearrange("p (c i t) -> p c t i", i=4, t=2), src.rearrange("p t (c i) -> p c t i", i=4))
 
-        def join(i, tag):
+        def join(i, place):
             copy, view = (nc.scalar.copy, U32) if i < SCALAR_JOINS else (nc.vector.tensor_copy, I32)
-            x_bf16[i] = pool.tile([P, 4 * PIECE], BF16, name=f"x_bf16_{i}", tag=tag, align_bytes=64)
+            x_bf16[i] = reused.tile([P, 4 * PIECE], BF16, name=f"x_bf16_{i}", offset=place, align_bytes=64)
             copy(x_bf16[i][:].bitcast(view).rearrange("p (s i u) -> p s u i", i=2, u=2), picked[:].bitcast(view)[:, :, entries(i)].rearrange("p u (s i) -> p s u i", i=2))
 
         def product(i):
@@ -82,25 +83,28 @@ def tile_picked_sidegate_sigmoid_l_kernel(tc, xT, side, w1, offs, out):
         for t in range(2):
             nc.vector.tensor_copy(pair0_halves[:, :, t], row[t][:].indirect(offsets[:]))
 
+        first_halves = picked[:, 1, entries(0)].bitcast(BF16).rearrange("p (s t) -> p s t", t=2)
+        nc.vector.tensor_copy(first_halves[:, :, 0], rows23[:, :T].indirect(listed(0)))
         for (lo, hi), share in zip(RANGES, SCALAR_SHARE):
             round_pair1(nc.scalar.copy, lo, lo + share)
             round_pair1(nc.vector.tensor_copy, lo + share, hi)
+        nc.vector.tensor_copy(first_halves[:, :, 1], rows23[:, T:].indirect(listed(0)))
         nc.scalar.copy(w_bf16[:].rearrange("p (c i t) -> p c t i", i=4, t=4), w_raw[:].rearrange("p t (c i) -> p c t i", i=4))
-        for i in range(PIECES):
+        for i in range(1, PIECES):
             nc.vector.tensor_copy(picked[:, 1, entries(i)], pair1_all[:].bitcast(U32).indirect(listed(i)))
 
-        join(0, "x_bf16_0")
-        join(1, "x_bf16_1")
+        join(0, 1024)
+        join(1, 3072)
         nc.vector.quantize_mx(out=w_codes[:].bitcast(FP8X4), scales=w_scales[:], in_=w_bf16[:])
-        join(2, "after_w_rounding")
+        join(2, 0)
         product(0)
-        join(3, "after_w_quantise")
+        join(3, 2048)
         for i in range(1, PIECES):
             product(i)
 
         for i in range(PIECES):
             nc.scalar.activation(gate[i][:], side_sb[:].indirect(listed(i)), SIGMOID)
         for i in range(PIECES):
-            result = pool.tile([P, PIECE], F32, name=f"result{i}", tag="after_w_rounding" if i == 0 else f"result{i}", align_bytes=64)
+            result = reused.tile([P, PIECE], F32, name=f"result{i}", offset=0 if i == 0 else 4096 + 512 * i, align_bytes=64)
             nc.vector.tensor_tensor(result[:], acc[i][:], gate[i][:], mybir.AluOpType.mult)
             nc.sync.dma_start(out[:, entries(i)], result[:])

@@ -37,7 +37,7 @@ def tile_picked_sidegate_sigmoid_l_kernel(tc, xT, side, w1, offs, out):
         row = [pool.tile([P, T], F32, name=f"row{t}") for t in range(2)]
         rows23 = pool.tile([P, 2 * T], F32, name="rows23")
         side_sb = pool.tile([P, T], F32, name="side_sb")
-        w_raw = reused.tile([P, 4, N], F32, name="w_raw", offset=0, align_bytes=64)
+        w_raw = reused.tile([P, 4, N], F32, name="w_raw", offset=1024, align_bytes=64)
         nc.sync.dma_start(row[0][:], x_rows[:, :T])
         nc.sync.dma_start(offsets[:], offs)
         nc.sync.dma_start(row[1][:], x_rows[:, T : 2 * T])
@@ -50,13 +50,13 @@ def tile_picked_sidegate_sigmoid_l_kernel(tc, xT, side, w1, offs, out):
 
         pair1_all = pool.tile([P, 2 * T], BF16, name="pair1_all", align_bytes=64)
         picked = pool.tile([P, 2, S], U32, name="picked")
-        x_codes = [pool.tile([P, PIECE], U32, name=f"x_codes{i}", align_bytes=64) for i in range(PIECES)]
+        x_codes = [reused.tile([P, PIECE], U32, name=f"x_codes{i}", offset=576 if i == 0 else 8192 + 512 * i, align_bytes=64) for i in range(PIECES)]
         x_scales = [pool.tile([P, PIECE], U8, name=f"x_scales{i}", align_bytes=64) for i in range(PIECES)]
         acc = [psum.tile([P, PIECE], F32, name=f"acc{i}") for i in range(PIECES)]
-        w_bf16 = reused.tile([P, 4 * N], BF16, name="w_bf16", offset=2048, align_bytes=64)
+        w_bf16 = reused.tile([P, 4 * N], BF16, name="w_bf16", offset=3200, align_bytes=64)
         w_codes = pool.tile([P, N], U32, name="w_codes", align_bytes=64)
         w_scales = pool.tile([P, N], U8, name="w_scales", align_bytes=64)
-        gate = [pool.tile([P, PIECE], F32, name=f"gate{i}") for i in range(PIECES)]
+        gate = pool.tile([P, S], F32, name="gate")
         x_bf16 = {}
 
         def entries(i):
@@ -70,7 +70,7 @@ def tile_picked_sidegate_sigmoid_l_kernel(tc, xT, side, w1, offs, out):
             copy(pair1_all[:, 2 * lo : 2 * hi].rearrange("p (c i t) -> p c t i", i=4, t=2), src.rearrange("p t (c i) -> p c t i", i=4))
 
         def join(i, place):
-            copy, view = (nc.scalar.copy, U32) if i < SCALAR_JOINS else (nc.vector.tensor_copy, I32)
+            copy, view = (nc.scalar.copy, U32) if i <= SCALAR_JOINS else (nc.vector.tensor_copy, I32)
             x_bf16[i] = reused.tile([P, 4 * PIECE], BF16, name=f"x_bf16_{i}", offset=place, align_bytes=64)
             copy(x_bf16[i][:].bitcast(view).rearrange("p (s i u) -> p s u i", i=2, u=2), picked[:].bitcast(view)[:, :, entries(i)].rearrange("p u (s i) -> p s u i", i=2))
 
@@ -80,31 +80,35 @@ def tile_picked_sidegate_sigmoid_l_kernel(tc, xT, side, w1, offs, out):
                                 rhs=x_codes[i][:].bitcast(FP8X4), rhs_scale=x_scales[i][:], start=True, stop=True)
 
         pair0_halves = picked[:, 0, :].bitcast(BF16).rearrange("p (s t) -> p s t", t=2)
+        first_pair0 = pool.tile([P, 2 * PIECE], BF16, name="first_pair0")
         for t in range(2):
-            nc.vector.tensor_copy(pair0_halves[:, :, t], row[t][:].indirect(offsets[:]))
+            nc.vector.tensor_copy(first_pair0[:].rearrange("p (s t) -> p s t", t=2)[:, :, t], row[t][:].indirect(listed(0)))
+            nc.vector.tensor_copy(pair0_halves[:, PIECE:, t], row[t][:].indirect(offsets[:, PIECE // 16 :]))
+        x_bf16[0] = pool.tile([P, 4 * PIECE], BF16, name="x_bf16_0", align_bytes=64)
+        nc.scalar.copy(x_bf16[0][:].bitcast(U32).rearrange("p (s u) -> p s u", u=2)[:, :, 0], first_pair0[:].bitcast(U32))
 
-        first_halves = picked[:, 1, entries(0)].bitcast(BF16).rearrange("p (s t) -> p s t", t=2)
-        nc.vector.tensor_copy(first_halves[:, :, 0], rows23[:, :T].indirect(listed(0)))
+        first_rows = x_bf16[0][:].rearrange("p (s t) -> p s t", t=4)
+        nc.vector.tensor_copy(first_rows[:, :, 2], rows23[:, :T].indirect(listed(0)))
         for (lo, hi), share in zip(RANGES, SCALAR_SHARE):
             round_pair1(nc.scalar.copy, lo, lo + share)
             round_pair1(nc.vector.tensor_copy, lo + share, hi)
-        nc.vector.tensor_copy(first_halves[:, :, 1], rows23[:, T:].indirect(listed(0)))
+        nc.vector.tensor_copy(first_rows[:, :, 3], rows23[:, T:].indirect(listed(0)))
         nc.scalar.copy(w_bf16[:].rearrange("p (c i t) -> p c t i", i=4, t=4), w_raw[:].rearrange("p t (c i) -> p c t i", i=4))
         for i in range(1, PIECES):
             nc.vector.tensor_copy(picked[:, 1, entries(i)], pair1_all[:].bitcast(U32).indirect(listed(i)))
 
-        join(0, 1024)
-        join(1, 3072)
+        join(1, 10752)
+        join(2, 11776)
         nc.vector.quantize_mx(out=w_codes[:].bitcast(FP8X4), scales=w_scales[:], in_=w_bf16[:])
-        join(2, 0)
         product(0)
-        join(3, 2048)
-        for i in range(1, PIECES):
-            product(i)
+        product(1)
+        join(3, 3200)
+        product(2)
+        product(3)
 
+        for lo, hi in ((0, 256), (256, 384), (384, 512)):
+            nc.scalar.activation(gate[:, lo:hi], side_sb[:].indirect(offsets[:, lo // 16 : hi // 16]), SIGMOID)
         for i in range(PIECES):
-            nc.scalar.activation(gate[i][:], side_sb[:].indirect(listed(i)), SIGMOID)
-        for i in range(PIECES):
-            result = reused.tile([P, PIECE], F32, name=f"result{i}", offset=0 if i == 0 else 4096 + 512 * i, align_bytes=64)
-            nc.vector.tensor_tensor(result[:], acc[i][:], gate[i][:], mybir.AluOpType.mult)
+            result = reused.tile([P, PIECE], F32, name=f"result{i}", offset=11776 if i == 0 else 5120 + 512 * i, align_bytes=64)
+            nc.vector.tensor_tensor(result[:], acc[i][:], gate[:, entries(i)], mybir.AluOpType.mult)
             nc.sync.dma_start(out[:, entries(i)], result[:])

@@ -15,8 +15,8 @@ SIGMOID = mybir.ActivationFunctionType.Sigmoid
 P = 128
 PIECE = 128
 PIECES = S // PIECE
-RANGES = [(0, 384), (384, 768), (768, 1024)]
-SCALAR_SHARE = [256, 128, 128]
+RANGES = [(0, 256), (256, 768), (768, 1024)]
+SCALAR_SHARE = [256, 192, 128]
 SCALAR_JOINS = 2
 
 
@@ -50,12 +50,14 @@ def tile_picked_sidegate_sigmoid_l_kernel(tc, xT, side, w1, offs, out):
 
         pair1_all = pool.tile([P, 2 * T], BF16, name="pair1_all", align_bytes=64)
         picked = pool.tile([P, 2, S], U32, name="picked")
-        x_codes = [reused.tile([P, PIECE], U32, name=f"x_codes{i}", offset=576 if i == 0 else 8192 + 512 * i, align_bytes=64) for i in range(PIECES)]
-        x_scales = [pool.tile([P, PIECE], U8, name=f"x_scales{i}", align_bytes=64) for i in range(PIECES)]
+        x_codes = {i: pool.tile([P, PIECE], U32, name=f"x_codes{i}", align_bytes=64) for i in range(1, PIECES)}
+        x_scales = {i: pool.tile([P, PIECE], U8, name=f"x_scales{i}", align_bytes=64) for i in range(1, PIECES)}
         acc = [psum.tile([P, PIECE], F32, name=f"acc{i}") for i in range(PIECES)]
-        w_bf16 = reused.tile([P, 4 * N], BF16, name="w_bf16", offset=3200, align_bytes=64)
-        w_codes = pool.tile([P, N], U32, name="w_codes", align_bytes=64)
-        w_scales = pool.tile([P, N], U8, name="w_scales", align_bytes=64)
+        w_and_first = pool.tile([P, 4 * (N + PIECE)], BF16, name="w_and_first", align_bytes=64)
+        w_bf16 = w_and_first[:, : 4 * N]
+        x_first = w_and_first[:, 4 * N :]
+        first_codes = pool.tile([P, N + PIECE], U32, name="first_codes", align_bytes=64)
+        first_scales = pool.tile([P, N + PIECE], U8, name="first_scales", align_bytes=64)
         gate = pool.tile([P, S], F32, name="gate")
         x_bf16 = {}
 
@@ -74,35 +76,38 @@ def tile_picked_sidegate_sigmoid_l_kernel(tc, xT, side, w1, offs, out):
             x_bf16[i] = reused.tile([P, 4 * PIECE], BF16, name=f"x_bf16_{i}", offset=place, align_bytes=64)
             copy(x_bf16[i][:].bitcast(view).rearrange("p (s i u) -> p s u i", i=2, u=2), picked[:].bitcast(view)[:, :, entries(i)].rearrange("p u (s i) -> p s u i", i=2))
 
+        def multiply(i, codes, scales):
+            nc.tensor.matmul_mx(out=acc[i][:], lhsT=first_codes[:, :N].bitcast(FP8X4), lhsT_scale=first_scales[:, :N],
+                                rhs=codes.bitcast(FP8X4), rhs_scale=scales, start=True, stop=True)
+
         def product(i):
             nc.vector.quantize_mx(out=x_codes[i][:].bitcast(FP8X4), scales=x_scales[i][:], in_=x_bf16[i][:])
-            nc.tensor.matmul_mx(out=acc[i][:], lhsT=w_codes[:].bitcast(FP8X4), lhsT_scale=w_scales[:],
-                                rhs=x_codes[i][:].bitcast(FP8X4), rhs_scale=x_scales[i][:], start=True, stop=True)
+            multiply(i, x_codes[i][:], x_scales[i][:])
 
         pair0_halves = picked[:, 0, :].bitcast(BF16).rearrange("p (s t) -> p s t", t=2)
         first_pair0 = pool.tile([P, 2 * PIECE], BF16, name="first_pair0")
         for t in range(2):
             nc.vector.tensor_copy(first_pair0[:].rearrange("p (s t) -> p s t", t=2)[:, :, t], row[t][:].indirect(listed(0)))
             nc.vector.tensor_copy(pair0_halves[:, PIECE:, t], row[t][:].indirect(offsets[:, PIECE // 16 :]))
-        x_bf16[0] = pool.tile([P, 4 * PIECE], BF16, name="x_bf16_0", align_bytes=64)
-        nc.scalar.copy(x_bf16[0][:].bitcast(U32).rearrange("p (s u) -> p s u", u=2)[:, :, 0], first_pair0[:].bitcast(U32))
+        nc.scalar.copy(x_first.bitcast(U32).rearrange("p (s u) -> p s u", u=2)[:, :, 0], first_pair0[:].bitcast(U32))
 
-        first_rows = x_bf16[0][:].rearrange("p (s t) -> p s t", t=4)
+        first_rows = x_first.rearrange("p (s t) -> p s t", t=4)
         nc.vector.tensor_copy(first_rows[:, :, 2], rows23[:, :T].indirect(listed(0)))
         for (lo, hi), share in zip(RANGES, SCALAR_SHARE):
             round_pair1(nc.scalar.copy, lo, lo + share)
-            round_pair1(nc.vector.tensor_copy, lo + share, hi)
+            if lo + share < hi:
+                round_pair1(nc.vector.tensor_copy, lo + share, hi)
         nc.vector.tensor_copy(first_rows[:, :, 3], rows23[:, T:].indirect(listed(0)))
-        nc.scalar.copy(w_bf16[:].rearrange("p (c i t) -> p c t i", i=4, t=4), w_raw[:].rearrange("p t (c i) -> p c t i", i=4))
+        nc.scalar.copy(w_bf16.rearrange("p (c i t) -> p c t i", i=4, t=4), w_raw[:].rearrange("p t (c i) -> p c t i", i=4))
         for i in range(1, PIECES):
             nc.vector.tensor_copy(picked[:, 1, entries(i)], pair1_all[:].bitcast(U32).indirect(listed(i)))
 
         join(1, 10752)
         join(2, 11776)
-        nc.vector.quantize_mx(out=w_codes[:].bitcast(FP8X4), scales=w_scales[:], in_=w_bf16[:])
-        product(0)
+        nc.vector.quantize_mx(out=first_codes[:].bitcast(FP8X4), scales=first_scales[:], in_=w_and_first[:])
+        multiply(0, first_codes[:, N:], first_scales[:, N:])
+        join(3, 1024)
         product(1)
-        join(3, 3200)
         product(2)
         product(3)
 

@@ -17,7 +17,7 @@ PIECE = 128
 PIECES = S // PIECE
 RANGES = [(0, 256), (256, 768), (768, 1024)]
 SCALAR_SHARE = [256, 192, 128]
-SCALAR_JOINS = 2
+SCALAR_JOIN_END = 320
 
 
 def tile_picked_sidegate_sigmoid_l_kernel(tc, xT, side, w1, offs, out):
@@ -59,7 +59,6 @@ def tile_picked_sidegate_sigmoid_l_kernel(tc, xT, side, w1, offs, out):
         first_codes = pool.tile([P, N + PIECE], U32, name="first_codes", align_bytes=64)
         first_scales = pool.tile([P, N + PIECE], U8, name="first_scales", align_bytes=64)
         gate = pool.tile([P, S], F32, name="gate")
-        x_bf16 = {}
 
         def entries(i):
             return slice(i * PIECE, (i + 1) * PIECE)
@@ -71,18 +70,15 @@ def tile_picked_sidegate_sigmoid_l_kernel(tc, xT, side, w1, offs, out):
             src = rows23[:].rearrange("p (t c) -> p t c", t=2)[:, :, lo:hi]
             copy(pair1_all[:, 2 * lo : 2 * hi].rearrange("p (c i t) -> p c t i", i=4, t=2), src.rearrange("p t (c i) -> p c t i", i=4))
 
-        def join(i, place):
-            copy, view = (nc.scalar.copy, U32) if i <= SCALAR_JOINS else (nc.vector.tensor_copy, I32)
-            x_bf16[i] = reused.tile([P, 4 * PIECE], BF16, name=f"x_bf16_{i}", offset=place, align_bytes=64)
-            copy(x_bf16[i][:].bitcast(view).rearrange("p (s i u) -> p s u i", i=2, u=2), picked[:].bitcast(view)[:, :, entries(i)].rearrange("p u (s i) -> p s u i", i=2))
+        def join(copy, view, dst, lo, hi):
+            copy(dst.bitcast(view).rearrange("p (s i u) -> p s u i", i=2, u=2), picked[:].bitcast(view)[:, :, lo:hi].rearrange("p u (s i) -> p s u i", i=2))
 
         def multiply(i, codes, scales):
             nc.tensor.matmul_mx(out=acc[i][:], lhsT=first_codes[:, :N].bitcast(FP8X4), lhsT_scale=first_scales[:, :N],
                                 rhs=codes.bitcast(FP8X4), rhs_scale=scales, start=True, stop=True)
 
-        def product(i):
-            nc.vector.quantize_mx(out=x_codes[i][:].bitcast(FP8X4), scales=x_scales[i][:], in_=x_bf16[i][:])
-            multiply(i, x_codes[i][:], x_scales[i][:])
+        def quantise(i, lo, hi, src):
+            nc.vector.quantize_mx(out=x_codes[i][:, lo:hi].bitcast(FP8X4), scales=x_scales[i][:, lo:hi], in_=src)
 
         pair0_halves = picked[:, 0, :].bitcast(BF16).rearrange("p (s t) -> p s t", t=2)
         first_pair0 = pool.tile([P, 2 * PIECE], BF16, name="first_pair0")
@@ -102,18 +98,25 @@ def tile_picked_sidegate_sigmoid_l_kernel(tc, xT, side, w1, offs, out):
         for i in range(1, PIECES):
             nc.vector.tensor_copy(picked[:, 1, entries(i)], pair1_all[:].bitcast(U32).indirect(listed(i)))
 
-        join(1, 10752)
-        join(2, 11776)
+        by_scalar = reused.tile([P, 4 * (SCALAR_JOIN_END - PIECE)], BF16, name="by_scalar", offset=10752, align_bytes=64)
+        by_vector = reused.tile([P, 4 * (S - SCALAR_JOIN_END)], BF16, name="by_vector", offset=1024, align_bytes=64)
+        join(nc.scalar.copy, U32, by_scalar[:, : 4 * PIECE], PIECE, 2 * PIECE)
+        join(nc.scalar.copy, U32, by_scalar[:, 4 * PIECE :], 2 * PIECE, SCALAR_JOIN_END)
         nc.vector.quantize_mx(out=first_codes[:].bitcast(FP8X4), scales=first_scales[:], in_=w_and_first[:])
         multiply(0, first_codes[:, N:], first_scales[:, N:])
-        join(3, 1024)
-        product(1)
-        product(2)
-        product(3)
+        join(nc.vector.tensor_copy, I32, by_vector[:], SCALAR_JOIN_END, S)
+        half = PIECE // 2
+        quantise(1, 0, PIECE, by_scalar[:, : 4 * PIECE])
+        multiply(1, x_codes[1][:], x_scales[1][:])
+        quantise(2, 0, half, by_scalar[:, 4 * PIECE :])
+        quantise(2, half, PIECE, by_vector[:, : 4 * half])
+        multiply(2, x_codes[2][:], x_scales[2][:])
+        quantise(3, 0, PIECE, by_vector[:, 4 * half :])
+        multiply(3, x_codes[3][:], x_scales[3][:])
 
         for lo, hi in ((0, 256), (256, 384), (384, 512)):
             nc.scalar.activation(gate[:, lo:hi], side_sb[:].indirect(offsets[:, lo // 16 : hi // 16]), SIGMOID)
         for i in range(PIECES):
-            result = reused.tile([P, PIECE], F32, name=f"result{i}", offset=11776 if i == 0 else 5120 + 512 * i, align_bytes=64)
+            result = reused.tile([P, PIECE], F32, name=f"result{i}", offset=10752 if i == 0 else 5120 + 512 * i, align_bytes=64)
             nc.vector.tensor_tensor(result[:], acc[i][:], gate[:, entries(i)], mybir.AluOpType.mult)
             nc.sync.dma_start(out[:, entries(i)], result[:])

@@ -7,17 +7,13 @@ FLOPS = 2 * K * S * N
 F32 = mybir.dt.float32
 BF16 = mybir.dt.bfloat16
 U32 = mybir.dt.uint32
-I32 = mybir.dt.int32
 U16 = mybir.dt.uint16
 U8 = mybir.dt.uint8
 FP8X4 = mybir.dt.float8_e4m3fn_x4
 SIGMOID = mybir.ActivationFunctionType.Sigmoid
+COPY = mybir.ActivationFunctionType.Copy
 P = 128
-PIECE = 128
-PIECES = S // PIECE
-RANGES = [(0, 256), (256, 768), (768, 1024)]
-SCALAR_SHARE = [256, 192, 128]
-SCALAR_JOIN_END = 320
+BY_SCALAR = 256
 
 
 def tile_picked_sidegate_sigmoid_l_kernel(tc, xT, side, w1, offs, out):
@@ -33,90 +29,61 @@ def tile_picked_sidegate_sigmoid_l_kernel(tc, xT, side, w1, offs, out):
         nc.vector.memset(warm_in[:], 0.0)
         nc.scalar.activation(warm_out[:], warm_in[:], SIGMOID)
 
-        x_rows = xT.rearrange("(p t) c -> p (t c)", t=4)
-        row = [pool.tile([P, T], F32, name=f"row{t}") for t in range(2)]
-        rows23 = pool.tile([P, 2 * T], F32, name="rows23")
+        x_rows = xT.rearrange("(p t) c -> p t c", t=4)
+        row = [pool.tile([P, T], F32, name=f"row{t}") for t in range(4)]
         side_sb = pool.tile([P, T], F32, name="side_sb")
-        w_raw = reused.tile([P, 4, N], F32, name="w_raw", offset=1024, align_bytes=64)
-        nc.sync.dma_start(row[0][:], x_rows[:, :T])
+        w_raw = reused.tile([P, 4 * N], F32, name="w_raw", offset=0, align_bytes=64)
+        nc.sync.dma_start(row[0][:], x_rows[:, 0, :])
         nc.sync.dma_start(offsets[:], offs)
-        nc.sync.dma_start(row[1][:], x_rows[:, T : 2 * T])
-        landed = 0
-        for lo, hi in RANGES:
-            nc.sync.dma_start(rows23[:, landed : T + hi], x_rows[:, 2 * T + landed : 3 * T + hi])
-            landed = T + hi
-        nc.sync.dma_start(w_raw[:], w1.rearrange("(p t) n -> p t n", t=4))
+        for t in range(1, 4):
+            nc.sync.dma_start(row[t][:], x_rows[:, t, :])
+        nc.sync.dma_start(w_raw[:], w1.rearrange("(p t) n -> p (t n)", t=4))
         nc.sync.dma_start(side_sb[:], side)
 
-        pair1_all = pool.tile([P, 2 * T], BF16, name="pair1_all", align_bytes=64)
-        picked = pool.tile([P, 2, S], U32, name="picked")
-        x_codes = {i: pool.tile([P, PIECE], U32, name=f"x_codes{i}", align_bytes=64) for i in range(1, PIECES)}
-        x_scales = {i: pool.tile([P, PIECE], U8, name=f"x_scales{i}", align_bytes=64) for i in range(1, PIECES)}
-        acc = [psum.tile([P, PIECE], F32, name=f"acc{i}") for i in range(PIECES)]
-        w_and_first = pool.tile([P, 4 * (N + PIECE)], BF16, name="w_and_first", align_bytes=64)
-        w_bf16 = w_and_first[:, : 4 * N]
-        x_first = w_and_first[:, 4 * N :]
-        first_codes = pool.tile([P, N + PIECE], U32, name="first_codes", align_bytes=64)
-        first_scales = pool.tile([P, N + PIECE], U8, name="first_scales", align_bytes=64)
+        def listed(lo, hi):
+            return offsets[:, lo // 16 : hi // 16]
+
+        planes = pool.tile([P, 4 * BY_SCALAR], F32, name="planes")
+        w_bf16 = pool.tile([P, 4 * N], BF16, name="w_bf16", align_bytes=64)
+        w_codes = pool.tile([P, N], U32, name="w_codes", align_bytes=64)
+        w_scales = pool.tile([P, N], U8, name="w_scales", align_bytes=64)
+        direct = pool.tile([P, 4 * (S - BY_SCALAR)], BF16, name="direct", align_bytes=64)
+        laid = pool.tile([P, 4 * BY_SCALAR], BF16, name="laid", align_bytes=64)
+        direct_rows = direct[:].rearrange("p (s t) -> p s t", t=4)
+        laid_rows = laid[:].rearrange("p (s t) -> p s t", t=4)
+        plane_rows = planes[:].rearrange("p (t s) -> p s t", t=4)
+        first = S - BY_SCALAR
+
+        for t in range(4):
+            cuts = [(0, 128), (128, 256)] if t == 3 else [(0, 256)]
+            for lo, hi in cuts:
+                nc.scalar.activation(planes[:, t * BY_SCALAR + lo : t * BY_SCALAR + hi], row[t][:].indirect(listed(first + lo, first + hi)), COPY)
+                nc.vector.tensor_copy(direct_rows[:, lo:hi, t], row[t][:].indirect(listed(lo, hi)))
+            if t % 2 == 1:
+                for lo, hi in cuts:
+                    nc.vector.tensor_copy(laid_rows[:, lo:hi, t - 1 : t + 1], plane_rows[:, lo:hi, t - 1 : t + 1])
+
+        nc.scalar.copy(w_bf16[:].rearrange("p (c i t) -> p c t i", i=4, t=4), w_raw[:].rearrange("p (t c i) -> p c t i", i=4, t=4))
+        nc.vector.quantize_mx(out=w_codes[:].bitcast(FP8X4), scales=w_scales[:], in_=w_bf16[:])
+        acc = [psum.tile([P, 256], F32, name=f"acc{half}") for half in range(2)]
+        for half, source in enumerate((direct, laid)):
+            if half == 1:
+                codes = reused.tile([P, 256], U32, name="codes_laid", offset=0, align_bytes=64)
+            else:
+                codes = pool.tile([P, 256], U32, name="codes_direct", align_bytes=64)
+            scales = pool.tile([P, 256], U8, name=f"scales{half}", align_bytes=64)
+            for lo, hi in ((0, 128), (128, 256)) if half == 0 else ((0, 256),):
+                nc.vector.quantize_mx(out=codes[:, lo:hi].bitcast(FP8X4), scales=scales[:, lo:hi], in_=source[:, 4 * lo : 4 * hi])
+            nc.tensor.matmul_mx(out=acc[half][:], lhsT=w_codes[:].bitcast(FP8X4), lhsT_scale=w_scales[:],
+                                rhs=codes[:].bitcast(FP8X4), rhs_scale=scales[:], start=True, stop=True)
+
         gate = pool.tile([P, S], F32, name="gate")
-
-        def entries(i):
-            return slice(i * PIECE, (i + 1) * PIECE)
-
-        def listed(i):
-            return offsets[:, i * PIECE // 16 : (i + 1) * PIECE // 16]
-
-        def round_pair1(copy, lo, hi):
-            src = rows23[:].rearrange("p (t c) -> p t c", t=2)[:, :, lo:hi]
-            copy(pair1_all[:, 2 * lo : 2 * hi].rearrange("p (c i t) -> p c t i", i=4, t=2), src.rearrange("p t (c i) -> p c t i", i=4))
-
-        def join(copy, view, dst, lo, hi):
-            copy(dst.bitcast(view).rearrange("p (s i u) -> p s u i", i=2, u=2), picked[:].bitcast(view)[:, :, lo:hi].rearrange("p u (s i) -> p s u i", i=2))
-
-        def multiply(i, codes, scales):
-            nc.tensor.matmul_mx(out=acc[i][:], lhsT=first_codes[:, :N].bitcast(FP8X4), lhsT_scale=first_scales[:, :N],
-                                rhs=codes.bitcast(FP8X4), rhs_scale=scales, start=True, stop=True)
-
-        def quantise(i, lo, hi, src):
-            nc.vector.quantize_mx(out=x_codes[i][:, lo:hi].bitcast(FP8X4), scales=x_scales[i][:, lo:hi], in_=src)
-
-        pair0_halves = picked[:, 0, :].bitcast(BF16).rearrange("p (s t) -> p s t", t=2)
-        first_pair0 = pool.tile([P, 2 * PIECE], BF16, name="first_pair0")
-        for t in range(2):
-            nc.vector.tensor_copy(first_pair0[:].rearrange("p (s t) -> p s t", t=2)[:, :, t], row[t][:].indirect(listed(0)))
-            nc.vector.tensor_copy(pair0_halves[:, PIECE:, t], row[t][:].indirect(offsets[:, PIECE // 16 :]))
-        nc.scalar.copy(x_first.bitcast(U32).rearrange("p (s u) -> p s u", u=2)[:, :, 0], first_pair0[:].bitcast(U32))
-
-        first_rows = x_first.rearrange("p (s t) -> p s t", t=4)
-        nc.vector.tensor_copy(first_rows[:, :, 2], rows23[:, :T].indirect(listed(0)))
-        for (lo, hi), share in zip(RANGES, SCALAR_SHARE):
-            round_pair1(nc.scalar.copy, lo, lo + share)
-            if lo + share < hi:
-                round_pair1(nc.vector.tensor_copy, lo + share, hi)
-        nc.vector.tensor_copy(first_rows[:, :, 3], rows23[:, T:].indirect(listed(0)))
-        nc.scalar.copy(w_bf16.rearrange("p (c i t) -> p c t i", i=4, t=4), w_raw[:].rearrange("p t (c i) -> p c t i", i=4))
-        for i in range(1, PIECES):
-            nc.vector.tensor_copy(picked[:, 1, entries(i)], pair1_all[:].bitcast(U32).indirect(listed(i)))
-
-        by_scalar = reused.tile([P, 4 * (SCALAR_JOIN_END - PIECE)], BF16, name="by_scalar", offset=10752, align_bytes=64)
-        by_vector = reused.tile([P, 4 * (S - SCALAR_JOIN_END)], BF16, name="by_vector", offset=1024, align_bytes=64)
-        join(nc.scalar.copy, U32, by_scalar[:, : 4 * PIECE], PIECE, 2 * PIECE)
-        join(nc.scalar.copy, U32, by_scalar[:, 4 * PIECE :], 2 * PIECE, SCALAR_JOIN_END)
-        nc.vector.quantize_mx(out=first_codes[:].bitcast(FP8X4), scales=first_scales[:], in_=w_and_first[:])
-        multiply(0, first_codes[:, N:], first_scales[:, N:])
-        join(nc.vector.tensor_copy, I32, by_vector[:], SCALAR_JOIN_END, S)
-        half = PIECE // 2
-        quantise(1, 0, PIECE, by_scalar[:, : 4 * PIECE])
-        multiply(1, x_codes[1][:], x_scales[1][:])
-        quantise(2, 0, half, by_scalar[:, 4 * PIECE :])
-        quantise(2, half, PIECE, by_vector[:, : 4 * half])
-        multiply(2, x_codes[2][:], x_scales[2][:])
-        quantise(3, 0, PIECE, by_vector[:, 4 * half :])
-        multiply(3, x_codes[3][:], x_scales[3][:])
-
-        for lo, hi in ((0, 256), (256, 384), (384, 512)):
-            nc.scalar.activation(gate[:, lo:hi], side_sb[:].indirect(offsets[:, lo // 16 : hi // 16]), SIGMOID)
-        for i in range(PIECES):
-            result = reused.tile([P, PIECE], F32, name=f"result{i}", offset=10752 if i == 0 else 5120 + 512 * i, align_bytes=64)
-            nc.vector.tensor_tensor(result[:], acc[i][:], gate[:, entries(i)], mybir.AluOpType.mult)
-            nc.sync.dma_start(out[:, entries(i)], result[:])
+        side_picked = pool.tile([P, 128], F32, name="side_picked")
+        nc.vector.tensor_copy(side_picked[:], side_sb[:].indirect(listed(384, S)))
+        for lo in (0, 128, 256):
+            nc.scalar.activation(gate[:, lo : lo + 128], side_sb[:].indirect(listed(lo, lo + 128)), SIGMOID)
+        nc.scalar.activation(gate[:, 384:], side_picked[:], SIGMOID)
+        for lo in range(0, S, 128):
+            result = pool.tile([P, 128], F32, name=f"result{lo}")
+            nc.vector.tensor_tensor(result[:], acc[lo // 256][:, lo % 256 : lo % 256 + 128], gate[:, lo : lo + 128], mybir.AluOpType.mult)
+            nc.sync.dma_start(out[:, lo : lo + 128], result[:])

@@ -60,21 +60,20 @@ def tile_picked_sidegate_sigmoid_l_kernel(tc, xT, side, w1, offs, out):
                 nc.scalar.activation(planes[:, t * BY_SCALAR + lo : t * BY_SCALAR + hi], row[t][:].indirect(listed(first + lo, first + hi)), COPY)
                 nc.vector.tensor_copy(direct_rows[:, lo:hi, t], row[t][:].indirect(listed(lo, hi)))
             if t % 2 == 1:
-                for lo, hi in cuts:
-                    nc.vector.tensor_copy(laid_rows[:, lo:hi, t - 1 : t + 1], plane_rows[:, lo:hi, t - 1 : t + 1])
+                nc.vector.tensor_copy(laid_rows[:, :128, t - 1 : t + 1], plane_rows[:, :128, t - 1 : t + 1])
+                lay = nc.scalar.copy if t == 1 else nc.vector.tensor_copy
+                lay(laid_rows[:, 128:, t - 1 : t + 1], plane_rows[:, 128:, t - 1 : t + 1])
 
         nc.scalar.copy(w_bf16[:].rearrange("p (c i t) -> p c t i", i=4, t=4), w_raw[:].rearrange("p (t c i) -> p c t i", i=4, t=4))
         nc.vector.quantize_mx(out=w_codes[:].bitcast(FP8X4), scales=w_scales[:], in_=w_bf16[:])
-        acc = [psum.tile([P, 256], F32, name=f"acc{half}") for half in range(2)]
-        for half, source in enumerate((direct, laid)):
-            if half == 1:
-                codes = reused.tile([P, 256], U32, name="codes_laid", offset=0, align_bytes=64)
-            else:
-                codes = pool.tile([P, 256], U32, name="codes_direct", align_bytes=64)
-            scales = pool.tile([P, 256], U8, name=f"scales{half}", align_bytes=64)
-            for lo, hi in ((0, 128), (128, 256)) if half == 0 else ((0, 256),):
-                nc.vector.quantize_mx(out=codes[:, lo:hi].bitcast(FP8X4), scales=scales[:, lo:hi], in_=source[:, 4 * lo : 4 * hi])
-            nc.tensor.matmul_mx(out=acc[half][:], lhsT=w_codes[:].bitcast(FP8X4), lhsT_scale=w_scales[:],
+        acc = []
+        for i in range(4):
+            source = direct if i < 2 else laid
+            codes = reused.tile([P, 128], U32, name=f"codes{i}", offset=2048 + 512 * i if i < 2 else 512 * i, align_bytes=64)
+            scales = pool.tile([P, 128], U8, name=f"scales{i}", align_bytes=64)
+            nc.vector.quantize_mx(out=codes[:].bitcast(FP8X4), scales=scales[:], in_=source[:, 512 * (i % 2) : 512 * (i % 2 + 1)])
+            acc.append(psum.tile([P, 128], F32, name=f"acc{i}"))
+            nc.tensor.matmul_mx(out=acc[i][:], lhsT=w_codes[:].bitcast(FP8X4), lhsT_scale=w_scales[:],
                                 rhs=codes[:].bitcast(FP8X4), rhs_scale=scales[:], start=True, stop=True)
 
         gate = pool.tile([P, S], F32, name="gate")
@@ -85,5 +84,5 @@ def tile_picked_sidegate_sigmoid_l_kernel(tc, xT, side, w1, offs, out):
         nc.scalar.activation(gate[:, 384:], side_picked[:], SIGMOID)
         for lo in range(0, S, 128):
             result = pool.tile([P, 128], F32, name=f"result{lo}")
-            nc.vector.tensor_tensor(result[:], acc[lo // 256][:, lo % 256 : lo % 256 + 128], gate[:, lo : lo + 128], mybir.AluOpType.mult)
+            nc.vector.tensor_tensor(result[:], acc[lo // 128][:], gate[:, lo : lo + 128], mybir.AluOpType.mult)
             nc.sync.dma_start(out[:, lo : lo + 128], result[:])

@@ -82,7 +82,7 @@ def tile_picked_sidegate_sigmoid_l_kernel(tc, xT, side, w1, offs, out):
         for lo in (0, 128, 256):
             nc.scalar.activation(gate[:, lo : lo + 128], side_sb[:].indirect(listed(lo, lo + 128)), SIGMOID)
         nc.scalar.activation(gate[:, 384:], side_picked[:], SIGMOID)
+        result = pool.tile([P, S], F32, name="result")
         for lo in range(0, S, 128):
-            result = pool.tile([P, 128], F32, name=f"result{lo}")
-            nc.vector.tensor_tensor(result[:], acc[lo // 128][:], gate[:, lo : lo + 128], mybir.AluOpType.mult)
-            nc.sync.dma_start(out[:, lo : lo + 128], result[:])
+            nc.vector.tensor_tensor(result[:, lo : lo + 128], acc[lo // 128][:], gate[:, lo : lo + 128], mybir.AluOpType.mult)
+        nc.sync.dma_start(out, result[:])

@@ -66,15 +66,15 @@ def tile_picked_sidegate_sigmoid_l_kernel(tc, xT, side, w1, offs, out):
 
         nc.scalar.copy(w_bf16[:].rearrange("p (c i t) -> p c t i", i=4, t=4), w_raw[:].rearrange("p (t c i) -> p c t i", i=4, t=4))
         nc.vector.quantize_mx(out=w_codes[:].bitcast(FP8X4), scales=w_scales[:], in_=w_bf16[:])
-        acc = []
-        for i in range(4):
-            source = direct if i < 2 else laid
-            codes = reused.tile([P, 128], U32, name=f"codes{i}", offset=2048 + 512 * i if i < 2 else 512 * i, align_bytes=64)
-            scales = pool.tile([P, 128], U8, name=f"scales{i}", align_bytes=64)
-            nc.vector.quantize_mx(out=codes[:].bitcast(FP8X4), scales=scales[:], in_=source[:, 512 * (i % 2) : 512 * (i % 2 + 1)])
-            acc.append(psum.tile([P, 128], F32, name=f"acc{i}"))
-            nc.tensor.matmul_mx(out=acc[i][:], lhsT=w_codes[:].bitcast(FP8X4), lhsT_scale=w_scales[:],
-                                rhs=codes[:].bitcast(FP8X4), rhs_scale=scales[:], start=True, stop=True)
+        acc = [psum.tile([P, 128], F32, name=f"acc{i}") for i in range(4)]
+        for lo, hi, source, offset in ((0, 128, direct[:, :512], 2048), (128, 256, direct[:, 512:], 2560), (256, 512, laid[:], 1024)):
+            codes = reused.tile([P, hi - lo], U32, name=f"codes{lo}", offset=offset, align_bytes=64)
+            scales = pool.tile([P, hi - lo], U8, name=f"scales{lo}", align_bytes=64)
+            nc.vector.quantize_mx(out=codes[:].bitcast(FP8X4), scales=scales[:], in_=source)
+            for at in range(lo, hi, 128):
+                cols = slice(at - lo, at - lo + 128)
+                nc.tensor.matmul_mx(out=acc[at // 128][:], lhsT=w_codes[:].bitcast(FP8X4), lhsT_scale=w_scales[:],
+                                    rhs=codes[:, cols].bitcast(FP8X4), rhs_scale=scales[:, cols], start=True, stop=True)
 
         gate = pool.tile([P, S], F32, name="gate")
         side_picked = pool.tile([P, 128], F32, name="side_picked")

from contextlib import ExitStack

import concourse.mybir as mybir

K, T, S, N = 512, 1024, 512, 128
FLOPS = 2 * K * S * N
F32 = mybir.dt.float32
BF16 = mybir.dt.bfloat16
U32 = mybir.dt.uint32
U16 = mybir.dt.uint16
U8 = mybir.dt.uint8
FP8X4 = mybir.dt.float8_e4m3fn_x4
SIGMOID = mybir.ActivationFunctionType.Sigmoid
COPY = mybir.ActivationFunctionType.Copy
P = 128
BY_SCALAR = 256


def tile_picked_sidegate_sigmoid_l_kernel(tc, xT, side, w1, offs, out):
    nc = tc.nc
    with ExitStack() as ctx:
        pool = ctx.enter_context(tc.tile_pool(name="pool", bufs=1))
        reused = ctx.enter_context(tc.tile_pool(name="reused", bufs=1))
        psum = ctx.enter_context(tc.psum_pool(name="psum", bufs=1))
        offsets = pool.tile([P, S // 16], U16, name="offsets")

        warm_in = pool.tile([P, 8], F32, name="warm_in")
        warm_out = pool.tile([P, 8], F32, name="warm_out")
        nc.vector.memset(warm_in[:], 0.0)
        nc.scalar.activation(warm_out[:], warm_in[:], SIGMOID)

        x_rows = xT.rearrange("(p t) c -> p t c", t=4)
        row = [pool.tile([P, T], F32, name=f"row{t}") for t in range(4)]
        side_sb = pool.tile([P, T], F32, name="side_sb")
        w_raw = reused.tile([P, 4 * N], F32, name="w_raw", offset=0, align_bytes=64)
        nc.sync.dma_start(row[0][:], x_rows[:, 0, :])
        nc.sync.dma_start(offsets[:], offs)
        for t in range(1, 4):
            nc.sync.dma_start(row[t][:], x_rows[:, t, :])
        nc.sync.dma_start(w_raw[:], w1.rearrange("(p t) n -> p (t n)", t=4))
        nc.sync.dma_start(side_sb[:], side)

        def listed(lo, hi):
            return offsets[:, lo // 16 : hi // 16]

        planes = pool.tile([P, 4 * BY_SCALAR], F32, name="planes")
        w_bf16 = pool.tile([P, 4 * N], BF16, name="w_bf16", align_bytes=64)
        w_codes = pool.tile([P, N], U32, name="w_codes", align_bytes=64)
        w_scales = pool.tile([P, N], U8, name="w_scales", align_bytes=64)
        direct = pool.tile([P, 4 * (S - BY_SCALAR)], BF16, name="direct", align_bytes=64)
        laid = pool.tile([P, 4 * BY_SCALAR], BF16, name="laid", align_bytes=64)
        direct_rows = direct[:].rearrange("p (s t) -> p s t", t=4)
        laid_rows = laid[:].rearrange("p (s t) -> p s t", t=4)
        plane_rows = planes[:].rearrange("p (t s) -> p s t", t=4)
        first = S - BY_SCALAR

        for t in range(4):
            cuts = [(0, 128), (128, 256)] if t == 3 else [(0, 256)]
            for lo, hi in cuts:
                nc.scalar.activation(planes[:, t * BY_SCALAR + lo : t * BY_SCALAR + hi], row[t][:].indirect(listed(first + lo, first + hi)), COPY)
                nc.vector.tensor_copy(direct_rows[:, lo:hi, t], row[t][:].indirect(listed(lo, hi)))
            if t % 2 == 1:
                nc.vector.tensor_copy(laid_rows[:, :128, t - 1 : t + 1], plane_rows[:, :128, t - 1 : t + 1])
                lay = nc.scalar.copy if t == 1 else nc.vector.tensor_copy
                lay(laid_rows[:, 128:, t - 1 : t + 1], plane_rows[:, 128:, t - 1 : t + 1])

        nc.scalar.copy(w_bf16[:].rearrange("p (c i t) -> p c t i", i=4, t=4), w_raw[:].rearrange("p (t c i) -> p c t i", i=4, t=4))
        nc.vector.quantize_mx(out=w_codes[:].bitcast(FP8X4), scales=w_scales[:], in_=w_bf16[:])
        acc = [psum.tile([P, 128], F32, name=f"acc{i}") for i in range(4)]
        for lo, hi, source, offset in ((0, 128, direct[:, :512], 2048), (128, 256, direct[:, 512:], 2560), (256, 512, laid[:], 1024)):
            codes = reused.tile([P, hi - lo], U32, name=f"codes{lo}", offset=offset, align_bytes=64)
            scales = pool.tile([P, hi - lo], U8, name=f"scales{lo}", align_bytes=64)
            nc.vector.quantize_mx(out=codes[:].bitcast(FP8X4), scales=scales[:], in_=source)
            for at in range(lo, hi, 128):
                cols = slice(at - lo, at - lo + 128)
                nc.tensor.matmul_mx(out=acc[at // 128][:], lhsT=w_codes[:].bitcast(FP8X4), lhsT_scale=w_scales[:],
                                    rhs=codes[:, cols].bitcast(FP8X4), rhs_scale=scales[:, cols], start=True, stop=True)

        gate = pool.tile([P, S], F32, name="gate")
        side_picked = pool.tile([P, 128], F32, name="side_picked")
        nc.vector.tensor_copy(side_picked[:], side_sb[:].indirect(listed(384, S)))
        for lo in (0, 128, 256):
            nc.scalar.activation(gate[:, lo : lo + 128], side_sb[:].indirect(listed(lo, lo + 128)), SIGMOID)
        nc.scalar.activation(gate[:, 384:], side_picked[:], SIGMOID)
        result = pool.tile([P, S], F32, name="result")
        for lo in range(0, S, 128):
            nc.vector.tensor_tensor(result[:, lo : lo + 128], acc[lo // 128][:], gate[:, lo : lo + 128], mybir.AluOpType.mult)
        nc.sync.dma_start(out, result[:])
